import numpy as np, ml_dtypes
CORES = [2,6,10,14,18,22,26,30]
N = 8
import mx_ref
BF = ml_dtypes.bfloat16
def entries(a):
    return np.ascontiguousarray(a.T).reshape(-1)
def table(e):
    return np.ascontiguousarray(np.reshape(e, (-1, 16)).T).astype(np.int32)
def cols(t, e):
    v = np.concatenate([t.reshape(128, -1, 4), np.zeros((128, 1, 4), BF)], axis=1)
    return np.ascontiguousarray(v[:, e]).reshape(128, -1)
def cut(t, i, w=512):
    return t[:, w * i:w * i + w]
def f(rng, *shape):
    return mx_ref.flush((rng.standard_normal(shape, dtype=np.float32) * np.exp2(rng.integers(-2, 3, shape[:-1] + (1,)))).astype(BF))
def wide(rng, *shape, cols=0):
    v = rng.standard_normal(shape, dtype=np.float32) * np.exp2(rng.integers(-12, 13, shape)).astype(np.float32)
    if cols: v *= np.repeat(np.exp2(rng.integers(-cols, cols + 1, shape[:-2] + (1, shape[-1] // 4))) * (rng.random(shape[:-2] + (1, shape[-1] // 4)) > 0.0625), 4, axis=-1).astype(np.float32)
    return mx_ref.flush(v.astype(BF))
K, B, R, O, CO = 256, 12, 5, 2, 56
def others(d):
    return [s for s in range(N) if s != d]
def numbers_of(a):
    return np.stack([entries(e) for e in a]).reshape(N, R, N, B)
def batch(tab, cs, t, d):
    return np.concatenate([cols(tab[s], cs[s, t, d]) for s in others(d)], axis=1)
def passes(u, new):
    return int(np.sum(mx_ref.matmul(mx_ref.quantize(u), mx_ref.quantize(new))[0] >= 0))
def write(tab, new, keys):
    tab.reshape(128, K, 4)[:, keys] = new.reshape(128, -1, 4)
def level(rng, n, rule, must):
    if rule == "all": return min(n)
    if rule == "none": return max(n) + 1
    if rule == "edge": return max(n)
    v = min(n, key=lambda a: abs(2 * sum(b >= a for b in n) - N))
    low = max([a for a in n if a < v], default=v - 1)
    h = int(rng.integers(low + 1, v + 1))
    return min(h, n[must]) if rule == "chain" else h
def draw_key(rng, at, got, d):
    for _ in range(1000):
        k = int(rng.integers(0, K)); q = divmod(int(at[k]), K)[0]
        if q == d or got[at[k]] or got.reshape(N, K)[q].sum() < CO:
            got[at[k]] = True
            return k
    raise RuntimeError("no key")
def draw_new(rng, at, got, d, q):
    k = np.flatnonzero((at >= q * K) & (at < q * K + K) & ~got[at])
    if len(k) == 0 or got.reshape(N, K)[q].sum() >= CO: return draw_key(rng, at, got, d)
    k = int(rng.choice(k)); got[at[k]] = True
    return k
def game(rng, x, u, rule):
    cs, cd, thr = np.full((N, R, N, B), -1), np.full((N, R, N, B), -1), np.zeros(16, int)
    tab, at = np.array(x, order="C"), np.arange(N * K).reshape(N, K)
    got = np.zeros((N, N * K), bool)
    p, hold, done = rng.permutation(N), rng.permutation(K)[:B], 0
    one, told = int(rng.integers(0, R)), {"all": 0, "none": (N - 1) * B + 1, "chain": (N - 1) * B}
    if rule == "chain":
        got[:, p[0] * K + hold] = True
        u[int(p[(one + 1) % N])] = 0
    for t in range(R):
        a, e = int(p[t % N]), int(p[(t + 1) % N])
        for d in range(N):
            cd[d, t, others(d)] = rng.permutation(K)[:(N - 1) * B].reshape(N - 1, B)
            for s in others(d):
                if rule == "chain" and (s, d) == (a, e): cs[s, t, d] = hold
                elif rule == "all" and d == p[0]: cs[s, t, d] = [draw_new(rng, at[s], got[d], d, int(p[1])) for j in range(B)]
                else: cs[s, t, d] = [draw_key(rng, at[s], got[d], d) for j in range(B)]
        new = [batch(tab, cs, t, d) for d in range(N)]
        src = [np.concatenate([at[s, cs[s, t, d]] for s in others(d)]) for d in range(N)]
        n = [passes(u[d], new[d]) for d in range(N)]
        thr[t] = told[rule] if t == one and rule in told else level(rng, n, rule, e)
        for d in range(N):
            if n[d] >= thr[t]:
                keys = cd[d, t, others(d)].reshape(-1)
                write(tab[d], new[d], keys); at[d, keys] = src[d]; done += 1
        hold = cd[e, t, a]
    return cs, cd, thr, done, int(got[p[0]].reshape(N, K)[p[1]].sum())
def make(rng, rule="half", x=None):
    if x is None: x = f(rng, N, 128, 4 * K)
    u = np.zeros((N, 128, 512), BF); u[:, :, :4] = f(rng, N, 128, 4)
    w = f(rng, N, 128, 512 * R * O)
    for _ in range(50):
        cs, cd, thr, done, most = game(rng, x, u, rule)
        if (rule != "half" or N * R <= 3 * done <= 2 * N * R) and (rule != "all" or most == CO):
            return {"x": x, "u": u, "w": w, "cs": np.stack([table(e.reshape(-1)) for e in cs]), "cd": np.stack([table(e.reshape(-1)) for e in cd]), "thr": np.stack([table(thr) for r in range(N)])}
    raise RuntimeError("no draw")
def setup_inputs(rng):
    return make(rng)
def setup_inputs_all(rng):
    return make(rng, "all")
def setup_inputs_none(rng):
    return make(rng, "none")
def setup_inputs_edge(rng):
    return make(rng, "edge")
def setup_inputs_chain(rng):
    return make(rng, "chain")
def setup_inputs_spread(rng):
    x = np.array(wide(rng, N, 128, 4 * K, cols=6))
    x[np.abs(x.astype(np.float32)) < 2.0 ** -30] = 0
    return make(rng, "half", x)
def check_inputs(d):
    b = []
    for name in ("x", "u", "w"):
        v = np.abs(np.asarray(d[name]).astype(np.float32))
        if not (np.isfinite(v) & ((v == 0) | ((v >= 2.0 ** -30) & (v <= 2.0 ** 30)))).all(): b.append(name + ": a value that isn't finite, or neither zero nor 2**-30 to 2**30 in size")
    cs, cd = numbers_of(d["cs"]), numbers_of(d["cd"])
    for r in range(N):
        for t in range(R):
            if (cs[r, t, r] != -1).any() or (cd[r, t, r] != -1).any(): b.append("a rank's own part isn't -1")
            k, e = cs[r, t, others(r)], cd[r, t, others(r)].reshape(-1)
            if k.min() < 0 or k.max() >= K: b.append("cs")
            if e.min() < 0 or e.max() >= K or len(set(e.tolist())) != len(e): b.append("cd")
        h = entries(d["thr"][r])
        if (h != entries(d["thr"][0])).any(): b.append("thr isn't the same on every rank")
        if h.min() < 0 or h.max() > (N - 1) * B + 1 or (h[R:] != 0).any(): b.append("thr")
    if (np.asarray(d["u"])[:, :, 4:].astype(np.float32) != 0).any(): b.append("u")
    if b: return b
    tab, at = np.array(d["x"], order="C"), np.arange(N * K).reshape(N, K)
    got = np.zeros((N, N * K), bool)
    for t in range(R):
        new = [batch(tab, cs, t, r) for r in range(N)]
        src = [np.concatenate([at[s, cs[s, t, r]] for s in others(r)]) for r in range(N)]
        for r in range(N):
            if passes(d["u"][r], new[r]) >= entries(d["thr"][r])[t]:
                keys = cd[r, t, others(r)].reshape(-1)
                write(tab[r], new[r], keys); at[r, keys] = src[r]; got[r, src[r]] = True
    for r in range(N):
        for q in others(r):
            if got[r].reshape(N, K)[q].sum() > CO: b.append("too many columns of one rank are written on another")
    return b
def reference(x, u, w, cs, cd, thr):
    cs, cd = numbers_of(cs), numbers_of(cd)
    tab = np.array(x, order="C")
    y = np.zeros((N, 128, R * O * K), np.float32)
    for t in range(R):
        new = [batch(tab, cs, t, d) for d in range(N)]
        for d in range(N):
            if passes(u[d], new[d]) >= entries(thr[d])[t]: write(tab[d], new[d], cd[d, t, others(d)].reshape(-1))
            q = mx_ref.quantize(tab[d])
            for o in range(O):
                i = t * O + o
                y[d][:, K * i:K * i + K] = mx_ref.matmul(mx_ref.quantize(cut(w[d], i)), q)
    return {"y": y}

@@ -1,0 +1,383 @@
+from concourse.bass import DstId, RemoteDMATransfer
+from concourse.mybir import dt, AluOpType, ActivationFunctionType
+
+N, K, B, R, O = 8, 256, 12, 5, 2
+NB = N * B
+NEW = (N - 1) * B
+LC = NB // 16
+TC = K // 16
+AL = R * LC
+WIN = K + 16
+STEP = 128
+TINY = 1e-30
+
+CODE, BYTE = "float8_e4m3fn_x4", "uint8"
+SCRATCH = {
+    "xt": ("sbuf", [128, 4 * K], "bfloat16"),
+    "ut": ("sbuf", [128, 512], "bfloat16"),
+    "wt": ("sbuf", [128, 512 * R * O], "bfloat16"),
+    "csl": ("sbuf", [128, AL], "int32"),
+    "cdl": ("sbuf", [128, AL], "int32"),
+    "thr1": ("sbuf", [1, 16], "int32"),
+    "thri": ("sbuf", [128, 16], "int32"),
+    "thrf": ("sbuf", [128, 16], "float32"),
+    "csu": ("sbuf", [128, AL], "uint16"),
+    "cdo": ("sbuf", [128, AL], "uint16"),
+    "own1": ("sbuf", [128, AL], "float32"),
+    "own2": ("sbuf", [128, AL], "float32"),
+    "cdf": ("sbuf", [128, AL], "float32"),
+    "trash": ("sbuf", [128, AL], "float32"),
+    "trash2": ("sbuf", [128, AL], "float32"),
+    "pp": ("sbuf", [128, 2], "int32"),
+    "p16": ("sbuf", [128, 2], "int32"),
+    "p16f": ("sbuf", [128, 2], "float32"),
+    "run": ("sbuf", [128, 384], "float32"),
+    "mask": ("sbuf", [128, 384], "float32"),
+    "seg": ("sbuf", [128, 384], "float32"),
+    "jc": ("sbuf", [128, TC], "float32"),
+    "jl": ("sbuf", [128, TC], "float32"),
+    "vrow": ("sbuf", [128, NB], "float32"),
+    "inv": ("sbuf", [128, R * WIN], "float32"),
+    "lists": ("sbuf", [128, AL + TC], "float32"),
+    "zeros": ("sbuf", [128, 8], "uint16"),
+    "uc": ("sbuf", [128, 128], CODE), "us": ("sbuf", [128, 128], BYTE),
+    "vc": ("sbuf", [128, 128], CODE), "vs": ("sbuf", [128, 128], BYTE),
+    "wc": ("sbuf", [128, 128 * R * O], CODE), "ws": ("sbuf", [128, 128 * R * O], BYTE),
+    "ttc": ("sbuf", [128, 2 * K], CODE), "tts": ("sbuf", [128, 2 * K], BYTE),
+    "ty": ("sbuf", [128, R * O * K], "float32"),
+    "acc": ("psum", [128, 1024], "float32"),
+    "prod": ("psum", [128, 2048], "float32"),
+    "fcf": ("sbuf", [128, TC], "float32"),
+    "fcu": ("sbuf", [128, TC], "uint16"),
+    "pkl": ("sbuf", [128, TC], "uint16"),
+}
+for _k in range(R + 1):
+    SCRATCH["pc%d" % _k] = ("sbuf", [128, K + NEW * _k], CODE)
+    SCRATCH["ps%d" % _k] = ("sbuf", [128, K + NEW * _k], BYTE)
+for _t in range(R):
+    SCRATCH["sc%d" % _t] = ("sbuf", [128, NB], CODE)
+    SCRATCH["ss%d" % _t] = ("sbuf", [128, NB], BYTE)
+    SCRATCH["val%d" % _t] = ("sbuf", [128, NB], "float32")
+    SCRATCH["lin%d" % _t] = ("sbuf", [128, 640], "float32")
+    SCRATCH["sum%d" % _t] = ("sbuf", [128, 640], "float32")
+    SCRATCH["bit%d" % _t] = ("sbuf", [128, NEW], "bfloat16")
+    SCRATCH["num%d" % _t] = ("sbuf", [128, 8], "float32")
+    SCRATCH["tmp%d" % _t] = ("sbuf", [128, AL + TC], "float32")
+    SCRATCH["lu%d" % _t] = ("sbuf", [128, AL + TC], "uint16")
+    if _t:
+        SCRATCH["cc%d" % _t] = ("sbuf", [128, STEP + NB], CODE)
+        SCRATCH["cs_%d" % _t] = ("sbuf", [128, STEP + NB], BYTE)
+        SCRATCH["ncf%d" % _t] = ("sbuf", [128, LC], "float32")
+        SCRATCH["ncu%d" % _t] = ("sbuf", [128, LC], "uint16")
+        SCRATCH["pk%d" % _t] = ("sbuf", [128, LC], "uint16")
+    if _t < R - 2 or _t == R - 1:
+        SCRATCH["tc%d" % _t] = ("sbuf", [128, K], CODE)
+        SCRATCH["ts%d" % _t] = ("sbuf", [128, K], BYTE)
+
+SEMAPHORES = ["vq", "aq", "pq", "gq", "lx0", "lx1", "lc0", "lc1", "ld0", "ld1", "lu", "lt", "yp"]
+for _t in range(R):
+    SEMAPHORES += ["arrc%d" % _t, "arrs%d" % _t, "yo%d" % _t, "snt%d" % _t, "lw%d" % _t]
+for _k in range(2, R + 1):
+    SEMAPHORES += ["cp%d" % _k]
+for _k in range(3, R + 1):
+    SEMAPHORES += ["co%d" % _k]
+
+
+def deal(topo, cores, s):
+    src = cores[s]
+    home, off = [], []
+    for d in range(len(cores)):
+        if d != s:
+            (home if topo.chip(cores[d]) == topo.chip(src) else off).append(d)
+    near = lambda d: topo.mates(topo.chip(src), topo.chip(cores[d])) or topo.same_plane(topo.chip(src), topo.chip(cores[d]))
+    eng = topo.engines(src, cores[off[0]])
+    even, odd = eng[0::2], eng[1::2]
+    two = len(eng) - len(off)
+    off = [d for d in off if not near(d)] + [d for d in off if near(d)]
+    codes, scales = {}, {}
+    for i, d in enumerate(off):
+        codes[d] = even[2 * i:2 * i + 2] if i < two else [odd[i - two]]
+        scales[d] = odd[2 * i:2 * i + 2] if i < two else [even[i - two]]
+    for d in home:
+        rest = [e for e in topo.engines(src, cores[d]) if e not in eng]
+        codes[d] = scales[d] = rest[::max(1, len(rest) // 2)][:2]
+    bits = lambda m: {d: sum(1 << e for e in m[d]) for d in m}
+    return bits(codes), bits(scales)
+
+
+def rank_program(g, core, T, topo):
+    r = T.rank_of(core)
+    if r is None:
+        return
+    cores = list(T.cores)
+    A, F = AluOpType, ActivationFunctionType
+    plans = [deal(topo, cores, s) for s in range(N)]
+    ones = lambda m: bin(m).count("1")
+
+    total, W, RD = {}, {}, {}
+    qs = {}
+    for name, eng, sem in (("v", g.vector, "vq"), ("a", g.scalar, "aq"), ("p", g.tensor, "pq"), ("g", g, "gq"), ("s", g.sync, None)):
+        qs[name] = {"eng": eng, "sem": sem, "seen": {}}
+
+    def hold(q, toks):
+        need = {}
+        for sem, n in toks:
+            n = total[sem] if n is None else n
+            if qs[q]["seen"].get(sem, 0) < n:
+                need[sem] = max(need.get(sem, 0), n)
+        for sem in sorted(need):
+            qs[q]["eng"].wait_ge(T.sem[sem], need[sem])
+            qs[q]["seen"][sem] = need[sem]
+
+    def order(q, rd, wr):
+        toks = []
+        for k in rd:
+            toks += W[k]
+        for k in wr:
+            toks += W.get(k, []) + RD.get(k, [])
+        hold(q, toks)
+
+    def note(tok, rd, wr):
+        for k in rd:
+            RD.setdefault(k, []).append(tok)
+        for k in wr:
+            W[k] = [tok]
+            RD[k] = []
+
+    def do(q, make, rd, wr):
+        order(q, rd, wr)
+        sem = qs[q]["sem"]
+        make(qs[q]["eng"]).then_inc(T.sem[sem], 1)
+        total[sem] = total.get(sem, 0) + 1
+        note((sem, total[sem]), rd, wr)
+
+    def dma(q, sem, out, in_, rd, wr):
+        order(q, rd, [])
+        qs[q]["eng"].dma_start(out, in_).then_inc(T.sem[sem], 16)
+        total[sem] = total.get(sem, 0) + 16
+        tok = (sem, None)
+        for k in rd:
+            RD.setdefault(k, []).append(tok)
+        for k in wr:
+            if tok not in W.setdefault(k, []):
+                W[k].append(tok)
+
+    for t in range(R):
+        for h, nm in ((0, "c"), (1, "s")):
+            sem = "arr%s%d" % (nm, t)
+            total[sem] = sum(ones(plans[s][h][r]) for s in range(N) if s != r)
+            W["land%s%d" % (nm, t)] = [(sem, None)]
+        W["sent%d" % t] = [("snt%d" % t, None)]
+
+    h = 2 * K
+    dma("s", "lx0", T.xt[:, 0:h], T.x[:, 0:h], [], ["x"])
+    dma("a", "lx1", T.xt[:, h:2 * h], T.x[:, h:2 * h], [], ["x"])
+    for i in range(8):
+        q, n = ("s", "0") if i < 4 else ("a", "1")
+        dma(q, "lc" + n, T.csl[16 * i:16 * i + 16, :], T.cs[:, :], [], ["cs"])
+    dma("s", "lu", T.ut[:, :], T.u[:, :], [], ["u"])
+    for i in range(8):
+        q, n = ("s", "0") if i < 4 else ("a", "1")
+        dma(q, "ld" + n, T.cdl[16 * i:16 * i + 16, :], T.cd[:, :], [], ["cd"])
+    dma("s", "lt", T.thr1[0:1, :], T.thr[:, :], [], ["thr1"])
+
+    fl = {"allow_small_or_imprecise_dtypes": True}
+    do("g", lambda e: e.iota(T.pp[:, 0:1], [[0, 1]], 0, 1), [], ["pp"])
+    do("g", lambda e: e.iota(T.run[:, :], [[0, 24], [1, 16]], 0, 0, **fl), [], ["run"])
+    do("g", lambda e: e.iota(T.jc[:, :], [[16, TC]], 0, 0, **fl), [], ["jc"])
+    do("g", lambda e: e.iota(T.trash[:, :], [[0, R], [16, LC]], K + 1 - B * r, 0, **fl), [], ["trash"])
+    do("g", lambda e: e.iota(T.vrow[:, 0:B * (r + 1)], [[1, B * (r + 1)]], 0, 0, **fl), [], ["vrowa"])
+    W["vrowb"] = []
+    if r < N - 1:
+        do("g", lambda e: e.iota(T.vrow[:, B * (r + 1):NB], [[1, NB - B * (r + 1)]], B * r, 0, **fl), [], ["vrowb"])
+    do("v", lambda e: e.memset(T.zeros[:, :], 0), [], ["zeros"])
+    for i in range(R):
+        do("v", lambda e: e.memset(T.inv[:, WIN * i:WIN * i + K], 0.0), [], ["inv%d" % i])
+    col = T.p16f[:, 0:1]
+    do("v", lambda e: e.tensor_scalar(T.p16[:, 0:1], T.pp[:, 0:1], 15, None, A.bitwise_and), ["pp"], ["p16"])
+    do("v", lambda e: e.tensor_copy(T.p16f[:, 0:1], T.p16[:, 0:1]), ["p16"], ["p16f"])
+    do("v", lambda e: e.tensor_scalar(T.mask[:, :], T.run[:, :], col, None, A.is_equal), ["run", "p16f"], ["mask"])
+    do("v", lambda e: e.tensor_scalar(T.jl[:, :], T.jc[:, :], col, None, A.add), ["jc", "p16f"], ["jl"])
+    do("v", lambda e: e.tensor_scalar(T.trash2[:, :], T.trash[:, :], col, None, A.add), ["trash", "p16f"], ["trash2"])
+    do("v", lambda e: e.tensor_copy(T.lists[:, AL:AL + TC], T.jl[:, :]), ["jl"], ["listb"])
+
+    def quantise(k):
+        do("v", lambda e: e.quantize_mx(T["pc%d" % k][:, 0:K], T["ps%d" % k][:, 0:K], T.xt[:, :]), ["x"], ["ownc%d" % k, "owns%d" % k])
+
+    def pick(q, nm, out, win, off, rd, wr):
+        if nm == "c":
+            do("v", lambda e: e.tensor_copy(T[out[0]][:, out[2]:out[3]].bitcast(dt.uint32), T[win[0]][:, win[2]:win[3]].bitcast(dt.uint32).indirect(off)), rd, wr)
+        elif q == "v":
+            do("v", lambda e: e.tensor_copy(T[out[1]][:, out[2]:out[3]], T[win[1]][:, win[2]:win[3]].indirect(off)), rd, wr)
+        else:
+            do("a", lambda e: e.activation(T[out[1]][:, out[2]:out[3]], T[win[1]][:, win[2]:win[3]].indirect(off), F.Copy), rd, wr)
+
+    def send(t):
+        codes, scales = plans[r]
+        for nm, m, scale in (("c", codes, False), ("s", scales, True)):
+            order("g", ["snd%s%d" % (nm, t)], [])
+            moves = []
+            for d in sorted(m):
+                rid, pid, _ring = topo.addr(cores[d])
+                a = K + NEW * t + B * (r - (r > d))
+                src = T["s%s%d" % (nm, t)][:, B * d:B * d + B]
+                dst = T["p%s%d" % (nm, t + 1)][:, a:a + B]
+                if not scale:
+                    src, dst = src.bitcast(dt.uint8), dst.bitcast(dt.uint8)
+                moves.append(RemoteDMATransfer(dst_ids=[DstId(rid=rid, pnc=pid)], dma_engine_mask=m[d], remote_sem=T.sem["arr%s%d" % (nm, t)], src=src, dst=dst))
+            sem = "snt%d" % t
+            g.remote_dma_fused(moves, local_sem=T.sem[sem])
+            total[sem] = total.get(sem, 0) + sum(ones(m[d]) for d in m)
+
+    def fetch(t):
+        a, b = 512 * O * t, 512 * O * (t + 1)
+        dma("s", "lw%d" % t, T.wt[:, a:b], T.w[:, a:b], ["sent%d" % max(t - 1, 0)], ["w%d" % t])
+
+    def carry(name, k, a, b, rd):
+        for nm in ("c", "s"):
+            o, i = T["p%s%d" % (nm, k)][:, a:b], T["p%s%d" % (nm, k - 1)][:, a:b]
+            if nm == "c":
+                o, i = o.bitcast(dt.uint8), i.bitcast(dt.uint8)
+            dma("s", "%s%d" % (name, k), o, i, rd(nm), ["%s%s%d" % (name, nm, k)])
+
+    quantise(0)
+    do("v", lambda e: e.tensor_copy(T.csu[:, :], T.csl[:, :]), ["cs"], ["csu"])
+    for nm in ("c", "s"):
+        pick("a", nm, ("sc0", "ss0", 0, NB), ("pc0", "ps0", 0, K), T.csu[:, 0:LC], ["own%s0" % nm, "csu"], ["snd%s0" % nm])
+    send(0)
+    fetch(0)
+    fetch(1)
+    do("g", lambda e: e.partition_broadcast(T.thri[:, :], T.thr1[0:1, :], 128), ["thr1"], ["thri"])
+
+    def later(t):
+        v, s, l, a = "val%d" % t, "sum%d" % t, "lin%d" % t, WIN * t
+        n = NB * (R - 1 - t)
+        do("v", lambda e: e.tensor_scalar(T[v][:, :], T.vrow[:, :], float(K + NEW * t), None, A.add), ["vrowa", "vrowb"], [v])
+        yield
+        do("v", lambda e: e.tensor_copy(T.inv[:, a:a + WIN].indirect(T.cdo[:, LC * t:LC * t + LC]), T[v][:, :]), [v, "cdo"], ["inv%d" % t])
+        yield
+        if n:
+            do("v", lambda e: e.tensor_tensor(T[l][:, 0:n], T.inv[:, a:a + K].indirect(T.csu[:, LC * (t + 1):AL]), T.mask[:, 0:n], A.mult), ["inv%d" % t, "csu", "mask"], [l + "a"])
+        do("v", lambda e: e.tensor_tensor(T[l][:, n:n + K], T.inv[:, a:a + K], T.mask[:, 0:K], A.mult), ["inv%d" % t, "mask"], [l + "b"])
+        if n:
+            do("v", lambda e: e.tensor_tensor_scan(T[s][:, 0:n], T.seg[:, 0:n], T[l][:, 0:n], 0.0, A.mult, A.add), ["seg", l + "a"], [s + "a"])
+        do("v", lambda e: e.tensor_tensor_scan(T[s][:, n:n + K], T.seg[:, 0:K], T[l][:, n:n + K], 0.0, A.mult, A.add), ["seg", l + "b"], [s + "b"])
+        yield
+
+    def newer(t):
+        do("v", lambda e: e.tensor_tensor(T["ncf%d" % t][:, :], T.lists[:, LC * t:LC * t + LC], T["sum%d" % (t - 1)][:, 15:16 * LC:16], A.max), ["lista", "sum%da" % (t - 1)], ["ncf%d" % t])
+        yield
+        do("v", lambda e: e.tensor_copy(T["ncu%d" % t][:, :], T["ncf%d" % t][:, :]), ["ncf%d" % t], ["ncu%d" % t])
+        yield
+
+    w0, n1 = later(0), newer(1)
+    quantise(1)
+    do("v", lambda e: e.tensor_scalar(T.own1[:, :], T.cdl[:, :], 0.0, None, A.is_lt), ["cd"], ["own1"])
+    do("v", lambda e: e.quantize_mx(T.uc[:, :], T.us[:, :], T.ut[:, :]), ["u"], ["uc", "us"])
+    do("v", lambda e: e.tensor_tensor(T.own2[:, :], T.own1[:, :], T.trash2[:, :], A.mult), ["own1", "trash2"], ["own2"])
+    for nm in ("c", "s"):
+        pick("a", nm, ("vc", "vs", 0, 128), ("uc", "us", 0, 128), T.zeros[:, :], ["u" + nm, "zeros"], ["v" + nm])
+    do("v", lambda e: e.tensor_tensor(T.cdf[:, :], T.cdl[:, :], T.own2[:, :], A.add), ["cd", "own2"], ["cdf"])
+    for nm in ("c", "s"):
+        pick("a", nm, ("cc1", "cs_1", 0, NB), ("pc1", "ps1", 0, K), T.csu[:, LC:2 * LC], ["own%s1" % nm, "csu"], ["nc%s1" % nm])
+    do("v", lambda e: e.tensor_copy(T.cdo[:, :], T.cdf[:, :]), ["cdf"], ["cdo"])
+    next(w0)
+    do("v", lambda e: e.tensor_scalar(T.lists[:, 0:AL], T.csl[:, :], 0.0, None, A.max), ["cs"], ["lista"])
+    next(w0)
+    do("v", lambda e: e.tensor_scalar(T.seg[:, :], T.run[:, :], 0.5, None, A.is_gt), ["run"], ["seg"])
+    next(w0)
+    next(n1)
+    do("v", lambda e: e.tensor_scalar(T.thrf[:, :], T.thri[:, :], 2.0, float(-NEW), A.mult, A.add), ["thri"], ["thrf"])
+    next(n1)
+
+    for t in range(R):
+        k = n = t + 1
+        end = K + NEW * k
+        num, bit = T["num%d" % t], T["bit%d" % t]
+        past = lambda x, j: (["cp%s%d" % (x, j)] if j > 1 else []) + (["co%s%d" % (x, j)] if j > 2 else [])
+        held = lambda x: ["own%s%d" % (x, k), "land%s%d" % (x, t)] + past(x, k)
+        if t < R - 1:
+            carry("cp", k + 1, end - NEW, end, lambda x: ["land%s%d" % (x, t)])
+        sb = 512 * (t % 2)
+        do("p", lambda e: e.matmul_mx(T.acc[:, sb:sb + 128], T.vc[:, :], T.vs[:, :], T["pc%d" % k][:, end - 128:end], T["ps%d" % k][:, end - 128:end], True, True), ["vc", "vs"] + held("c") + held("s"), ["acc%d" % (t % 2)])
+        if t < R - 1:
+            out, off, cv = ("cc%d" % n, "cs_%d" % n, STEP, STEP + NB), T["ncu%d" % n][:, :], "ncu%d" % n
+        else:
+            out, off, cv = ("ttc", "tts", K, 2 * K), T.fcu[:, :], "fcu"
+        win = ("pc%d" % k, "ps%d" % k, 0, end)
+        for nm in ("c", "s"):
+            pick("v", nm, out, win, off, held(nm) + [cv], ["wc%s%d" % (nm, n)])
+        do("a", lambda e: e.activation(bit[:, :], T.acc[:, sb + 128 - NEW:sb + 128], F.Sign, bias=TINY, accum_out=num[:, 0:1]), ["acc%d" % (t % 2)], ["cnt%d" % t])
+        step, width = (STEP, LC) if t < R - 1 else (K, TC)
+        do("v", lambda e: e.tensor_scalar(num[:, 4:5], num[:, 0:1], T.thrf[:, t:t + 1], float(step), A.is_ge, A.mult), ["cnt%d" % t, "thrf"], ["shift%d" % t])
+        pkl = T["pk%d" % n] if t < R - 1 else T.pkl
+        do("v", lambda e: e.tensor_scalar(pkl[:, :], T.jl[:, 0:width], num[:, 4:5], None, A.add), ["jl", "shift%d" % t], ["pk%d" % n])
+        if t < R - 1:
+            src, dst = ("cc%d" % n, "cs_%d" % n, 0, STEP + NB), ("sc%d" % n, "ss%d" % n, 0, NB)
+            for nm in ("c", "s"):
+                pick("a", nm, dst, src, pkl[:, :], ["nc%s%d" % (nm, n), "wc%s%d" % (nm, n), "pk%d" % n], ["snd%s%d" % (nm, n)])
+            send(n)
+            wn = later(n)
+            lo = LC * (t + 2)
+            wid = AL + TC - lo
+            tmp, lu, sm = T["tmp%d" % t], T["lu%d" % t], T["sum%d" % t]
+            do("v", lambda e: e.tensor_scalar(tmp[:, 0:wid], sm[:, 16 * LC + 15:16 * (LC + wid):16], num[:, 4:5], 1.0 / STEP, A.mult, A.mult), ["sum%da" % t, "sum%db" % t, "shift%d" % t], ["tmp%d" % t])
+            next(wn)
+            do("v", lambda e: e.tensor_tensor(T.lists[:, lo:AL + TC], T.lists[:, lo:AL + TC], tmp[:, 0:wid], A.max), ["tmp%d" % t, "lista", "listb"], ["lista", "listb"])
+            next(wn)
+            do("v", lambda e: e.tensor_copy(lu[:, lo:AL + TC], T.lists[:, lo:AL + TC]), ["lista", "listb"], ["lu%d" % t])
+            for i in [t] + ([n] if t == R - 2 else []):
+                a, b = 128 * O * i, 128 * O * (i + 1)
+                do("v", lambda e: e.quantize_mx(T.wc[:, a:b], T.ws[:, a:b], T.wt[:, 4 * a:4 * b]), ["w%d" % i], ["wq%d" % i])
+            tab = ("tc%d" % t, "ts%d" % t, 0, K) if t < R - 2 else ("ttc", "tts", 0, K)
+            for nm in ("c", "s"):
+                pick("a", nm, tab, win, lu[:, AL:AL + TC], held(nm) + ["lu%d" % t], ["tab%s%d" % (nm, t)])
+            for o in range(O):
+                i = O * t + o
+                pb = 512 * (i % 4)
+                do("p", lambda e: e.matmul_mx(T.prod[:, pb:pb + K], T.wc[:, 128 * i:128 * i + 128], T.ws[:, 128 * i:128 * i + 128], T[tab[0]][:, 0:K], T[tab[1]][:, 0:K], True, True), ["wq%d" % t, "tabc%d" % t, "tabs%d" % t], ["prod%d" % (i % 4)])
+            for o in range(O):
+                i = O * t + o
+                pb = 512 * (i % 4)
+                do("a", lambda e: e.activation(T.ty[:, K * i:K * i + K], T.prod[:, pb:pb + K], F.Copy), ["prod%d" % (i % 4)], ["ty%d" % i])
+            if n + 1 < R:
+                fetch(n + 1)
+            if k + 2 <= R:
+                carry("co", k + 2, K, end, lambda x: ["sent%d" % n] + past(x, k + 1))
+            y = slice(O * K * t, O * K * (t + 1))
+            dma("s", "yo%d" % t, T.y[:, y], T.ty[:, y], ["sent%d" % n, "ty%d" % (O * t), "ty%d" % (O * t + 1)], ["out%d" % t])
+            next(wn)
+            quantise(k + 1)
+            if t < R - 2:
+                m = n + 1
+                nw = newer(m)
+                next(nw)
+                src = ("pc%d" % (k + 1), "ps%d" % (k + 1), 0, end)
+                for nm in ("c", "s"):
+                    pick("a", nm, ("cc%d" % m, "cs_%d" % m, 0, NB), src, lu[:, LC * m:LC * m + LC], ["own%s%d" % (nm, k + 1), "lu%d" % t] + past(nm, k + 1), ["nc%s%d" % (nm, m)])
+                next(nw)
+            else:
+                do("v", lambda e: e.tensor_tensor(T.fcf[:, :], T.lists[:, AL:AL + TC], T["sum%d" % n][:, 15:16 * TC:16], A.max), ["listb", "sum%db" % n], ["fcf"])
+                do("v", lambda e: e.tensor_copy(T.fcu[:, :], T.fcf[:, :]), ["fcf"], ["fcu"])
+        else:
+            H = K // 2
+            for h in range(2):
+                tab = ("tc%d" % t, "ts%d" % t, H * h, H * h + H)
+                for nm in ("c", "s"):
+                    pick("a", nm, tab, ("ttc", "tts", 0, 2 * K), pkl[:, TC // 2 * h:TC // 2 * (h + 1)], ["tab%s%d" % (nm, t - 1), "wc%s%d" % (nm, n), "pk%d" % n], ["tab%s%d%d" % (nm, t, h)])
+                for o in range(O):
+                    i = O * t + o
+                    pb = 512 * (2 * h + o)
+                    do("p", lambda e: e.matmul_mx(T.prod[:, pb:pb + H], T.wc[:, 128 * i:128 * i + 128], T.ws[:, 128 * i:128 * i + 128], T[tab[0]][:, tab[2]:tab[3]], T[tab[1]][:, tab[2]:tab[3]], True, True), ["wq%d" % t, "tabc%d%d" % (t, h), "tabs%d%d" % (t, h)], ["prod%d" % (2 * h + o)])
+            for h in range(2):
+                for o in range(O):
+                    a, pb = K * (O * t + o) + H * h, 512 * (2 * h + o)
+                    y = slice(a, a + H)
+                    if o:
+                        do("a", lambda e: e.activation(T.ty[:, y], T.prod[:, pb:pb + H], F.Copy), ["prod%d" % (2 * h + o)], ["tyz%d%d" % (h, o)])
+                    else:
+                        do("v", lambda e: e.tensor_copy(T.ty[:, y], T.prod[:, pb:pb + H]), ["prod%d" % (2 * h + o)], ["tyz%d%d" % (h, o)])
+                    q, sem = ("a", "yp") if o and h else ("s", "yo%d" % t)
+                    dma(q, sem, T.y[:, y], T.ty[:, y], ["tyz%d%d" % (h, o)], ["outz%d%d" % (h, o)])
+
+    hold("g", [(sem, None) for sem in sorted(total)])

@@ -4,83 +4,66 @@ from concourse.mybir import dt, AluOpType, ActivationFunctionType
 N, K, B, R, O = 8, 256, 12, 5, 2
 NB = N * B
 NEW = (N - 1) * B
+END = K + NEW
 LC = NB // 16
 TC = K // 16
 AL = R * LC
-WIN = K + 16
-STEP = 128
+RW = TC + 2 * LC + 2
+SPAN = 256
 TINY = 1e-30
 
 CODE, BYTE = "float8_e4m3fn_x4", "uint8"
+F32, I32, U16 = "float32", "int32", "uint16"
 SCRATCH = {
     "xt": ("sbuf", [128, 4 * K], "bfloat16"),
     "ut": ("sbuf", [128, 512], "bfloat16"),
     "wt": ("sbuf", [128, 512 * R * O], "bfloat16"),
-    "csl": ("sbuf", [128, AL], "int32"),
-    "cdl": ("sbuf", [128, AL], "int32"),
-    "thr1": ("sbuf", [1, 16], "int32"),
-    "thri": ("sbuf", [128, 16], "int32"),
-    "thrf": ("sbuf", [128, 16], "float32"),
-    "csu": ("sbuf", [128, AL], "uint16"),
-    "cdo": ("sbuf", [128, AL], "uint16"),
-    "own1": ("sbuf", [128, AL], "float32"),
-    "own2": ("sbuf", [128, AL], "float32"),
-    "cdf": ("sbuf", [128, AL], "float32"),
-    "trash": ("sbuf", [128, AL], "float32"),
-    "trash2": ("sbuf", [128, AL], "float32"),
-    "pp": ("sbuf", [128, 2], "int32"),
-    "p16": ("sbuf", [128, 2], "int32"),
-    "p16f": ("sbuf", [128, 2], "float32"),
-    "run": ("sbuf", [128, 384], "float32"),
-    "mask": ("sbuf", [128, 384], "float32"),
-    "seg": ("sbuf", [128, 384], "float32"),
-    "jc": ("sbuf", [128, TC], "float32"),
-    "jl": ("sbuf", [128, TC], "float32"),
-    "vrow": ("sbuf", [128, NB], "float32"),
-    "inv": ("sbuf", [128, R * WIN], "float32"),
-    "lists": ("sbuf", [128, AL + TC], "float32"),
-    "zeros": ("sbuf", [128, 8], "uint16"),
+    "csl": ("sbuf", [128, AL], I32), "cdg": ("sbuf", [128, LC], I32),
+    "cs0": ("sbuf", [128, LC], U16),
+    "thr1": ("sbuf", [1, 16], I32), "thri": ("sbuf", [128, 16], I32), "thrf": ("sbuf", [128, 16], F32),
+    "pp": ("sbuf", [128, 2], I32), "p16": ("sbuf", [128, 2], I32), "pg": ("sbuf", [128, 2], I32),
+    "pq": ("sbuf", [128, 4], I32),
+    "colf": ("sbuf", [128, 8], F32),
+    "nxt": ("sbuf", [128, 2], U16),
+    "jc": ("sbuf", [128, R * TC], F32),
+    "ent": ("sbuf", [128, 5 * LC], F32), "kt": ("sbuf", [128, LC], F32),
+    "thrg": ("sbuf", [128, 16], F32), "base": ("sbuf", [128, R * LC], F32),
+    "spf": ("sbuf", [128, 2 * LC], F32), "spu": ("sbuf", [128, 2 * LC], U16),
+    "kp": ("sbuf", [128, LC + 16], I32), "kb": ("sbuf", [128, 2 * LC], I32),
+    "k1": ("sbuf", [128, 2 * LC], F32), "k2": ("sbuf", [128, 2 * LC], F32), "k3": ("sbuf", [128, 2 * LC], F32),
+    "po": ("sbuf", [128, 2 * LC], U16),
+    "vrow": ("sbuf", [128, NB], F32), "grow": ("sbuf", [128, 2 * NB], F32),
+    "row": ("sbuf", [128, 16 * RW], F32),
+    "bl": ("sbuf", [128, R * RW], F32),
+    "both": ("sbuf", [128, 2 * R * TC], F32),
+    "zeros": ("sbuf", [128, 8], U16),
     "uc": ("sbuf", [128, 128], CODE), "us": ("sbuf", [128, 128], BYTE),
     "vc": ("sbuf", [128, 128], CODE), "vs": ("sbuf", [128, 128], BYTE),
     "wc": ("sbuf", [128, 128 * R * O], CODE), "ws": ("sbuf", [128, 128 * R * O], BYTE),
-    "ttc": ("sbuf", [128, 2 * K], CODE), "tts": ("sbuf", [128, 2 * K], BYTE),
-    "ty": ("sbuf", [128, R * O * K], "float32"),
-    "acc": ("psum", [128, 1024], "float32"),
-    "prod": ("psum", [128, 2048], "float32"),
-    "fcf": ("sbuf", [128, TC], "float32"),
-    "fcu": ("sbuf", [128, TC], "uint16"),
-    "pkl": ("sbuf", [128, TC], "uint16"),
+    "xc": ("sbuf", [128, K], CODE), "xs": ("sbuf", [128, K], BYTE),
+    "ty": ("sbuf", [128, R * O * K], F32),
+    "acc": ("psum", [128, 1024], F32),
+    "prod": ("psum", [128, 2048], F32),
 }
-for _k in range(R + 1):
-    SCRATCH["pc%d" % _k] = ("sbuf", [128, K + NEW * _k], CODE)
-    SCRATCH["ps%d" % _k] = ("sbuf", [128, K + NEW * _k], BYTE)
+for _t in range(R + 1):
+    SCRATCH["lc%d" % _t] = ("sbuf", [128, END if _t < R else K], CODE)
+    SCRATCH["ls%d" % _t] = ("sbuf", [128, END if _t < R else K], BYTE)
 for _t in range(R):
     SCRATCH["sc%d" % _t] = ("sbuf", [128, NB], CODE)
     SCRATCH["ss%d" % _t] = ("sbuf", [128, NB], BYTE)
-    SCRATCH["val%d" % _t] = ("sbuf", [128, NB], "float32")
-    SCRATCH["lin%d" % _t] = ("sbuf", [128, 640], "float32")
-    SCRATCH["sum%d" % _t] = ("sbuf", [128, 640], "float32")
     SCRATCH["bit%d" % _t] = ("sbuf", [128, NEW], "bfloat16")
-    SCRATCH["num%d" % _t] = ("sbuf", [128, 8], "float32")
-    SCRATCH["tmp%d" % _t] = ("sbuf", [128, AL + TC], "float32")
-    SCRATCH["lu%d" % _t] = ("sbuf", [128, AL + TC], "uint16")
-    if _t:
-        SCRATCH["cc%d" % _t] = ("sbuf", [128, STEP + NB], CODE)
-        SCRATCH["cs_%d" % _t] = ("sbuf", [128, STEP + NB], BYTE)
-        SCRATCH["ncf%d" % _t] = ("sbuf", [128, LC], "float32")
-        SCRATCH["ncu%d" % _t] = ("sbuf", [128, LC], "uint16")
-        SCRATCH["pk%d" % _t] = ("sbuf", [128, LC], "uint16")
-    if _t < R - 2 or _t == R - 1:
-        SCRATCH["tc%d" % _t] = ("sbuf", [128, K], CODE)
-        SCRATCH["ts%d" % _t] = ("sbuf", [128, K], BYTE)
+    SCRATCH["num%d" % _t] = ("sbuf", [128, 2], F32)
+    SCRATCH["sel%d" % _t] = ("sbuf", [128, 2], U16)
+    SCRATCH["tl%d" % _t] = ("sbuf", [128, TC], U16)
+    if _t < R - 1:
+        SCRATCH["nl%d" % _t] = ("sbuf", [128, 2 * LC], U16)
+        SCRATCH["pk%d" % _t] = ("sbuf", [128, LC], U16)
+        SCRATCH["cc%d" % _t] = ("sbuf", [128, 2 * NB], CODE)
+        SCRATCH["cs%dx" % _t] = ("sbuf", [128, 2 * NB], BYTE)
 
-SEMAPHORES = ["vq", "aq", "pq", "gq", "lx0", "lx1", "lc0", "lc1", "ld0", "ld1", "lu", "lt", "yp"]
+SEMAPHORES = ["vq", "aq", "pq", "gq", "lx0", "lx1", "lcs", "lcd", "lu", "lt", "yp", "lb0", "lb1"]
 for _t in range(R):
-    SEMAPHORES += ["arrc%d" % _t, "arrs%d" % _t, "yo%d" % _t, "snt%d" % _t, "lw%d" % _t]
-for _k in range(2, R + 1):
-    SEMAPHORES += ["cp%d" % _k]
-for _k in range(3, R + 1):
-    SEMAPHORES += ["co%d" % _k]
+    SEMAPHORES += ["snt%d" % _t, "arr%d" % _t, "yo%d" % _t, "lw%d" % _t]
 
 
 def deal(topo, cores, s):
@@ -125,7 +108,7 @@ def rank_program(g, core, T, topo):
             n = total[sem] if n is None else n
             if qs[q]["seen"].get(sem, 0) < n:
                 need[sem] = max(need.get(sem, 0), n)
-        for sem in sorted(need):
+        for sem in sorted(need, key=lambda s: (s.startswith("arr"), s)):
             qs[q]["eng"].wait_ge(T.sem[sem], need[sem])
             qs[q]["seen"][sem] = need[sem]
 
@@ -162,213 +145,196 @@ def rank_program(g, core, T, topo):
             if tok not in W.setdefault(k, []):
                 W[k].append(tok)
 
+    def ts(out, in0, s1, op0, rd, wr, s2=None, op1=None):
+        if op1 is None:
+            do("v", lambda e: e.tensor_scalar(out, in0, s1, None, op0), rd, wr)
+        else:
+            do("v", lambda e: e.tensor_scalar(out, in0, s1, s2, op0, op1), rd, wr)
+
+    def tt(out, in0, in1, op, rd, wr):
+        do("v", lambda e: e.tensor_tensor(out, in0, in1, op), rd, wr)
+
+    def cp(out, in_, rd, wr):
+        do("v", lambda e: e.tensor_copy(out, in_), rd, wr)
+
     for t in range(R):
-        for h, nm in ((0, "c"), (1, "s")):
-            sem = "arr%s%d" % (nm, t)
-            total[sem] = sum(ones(plans[s][h][r]) for s in range(N) if s != r)
-            W["land%s%d" % (nm, t)] = [(sem, None)]
-        W["sent%d" % t] = [("snt%d" % t, None)]
+        total["arr%d" % t] = sum(ones(plans[s][h][r]) for s in range(N) if s != r for h in range(2))
+        W["land%d" % t] = [("arr%d" % t, None)]
 
     h = 2 * K
-    dma("s", "lx0", T.xt[:, 0:h], T.x[:, 0:h], [], ["x"])
-    dma("a", "lx1", T.xt[:, h:2 * h], T.x[:, h:2 * h], [], ["x"])
+    dma("s", "lx0", T.xt[:, 0:h], T.x[:, 0:h], [], ["x0"])
+    dma("s", "lx1", T.xt[:, h:2 * h], T.x[:, h:2 * h], [], ["x1"])
     for i in range(8):
-        q, n = ("s", "0") if i < 4 else ("a", "1")
-        dma(q, "lc" + n, T.csl[16 * i:16 * i + 16, :], T.cs[:, :], [], ["cs"])
-    dma("s", "lu", T.ut[:, :], T.u[:, :], [], ["u"])
+        dma("a" if i < 5 else "s", "lcs", T.csl[16 * i:16 * i + 16, :], T.cs[:, :], [], ["cs"])
+    dma("a", "lt", T.thr1[0:1, :], T.thr[:, :], [], ["thr1"])
     for i in range(8):
-        q, n = ("s", "0") if i < 4 else ("a", "1")
-        dma(q, "ld" + n, T.cdl[16 * i:16 * i + 16, :], T.cd[:, :], [], ["cd"])
-    dma("s", "lt", T.thr1[0:1, :], T.thr[:, :], [], ["thr1"])
+        t = min(i, R - 1)
+        dma("sa"[i % 2], "lcd", T.cdg[16 * i:16 * i + 16, :], T.cd[:, LC * t:LC * t + LC], [], ["cd"])
+    dma("s", "lu", T.ut[:, 0:8], T.u[:, 0:8], [], ["u"])
 
     fl = {"allow_small_or_imprecise_dtypes": True}
     do("g", lambda e: e.iota(T.pp[:, 0:1], [[0, 1]], 0, 1), [], ["pp"])
-    do("g", lambda e: e.iota(T.run[:, :], [[0, 24], [1, 16]], 0, 0, **fl), [], ["run"])
-    do("g", lambda e: e.iota(T.jc[:, :], [[16, TC]], 0, 0, **fl), [], ["jc"])
-    do("g", lambda e: e.iota(T.trash[:, :], [[0, R], [16, LC]], K + 1 - B * r, 0, **fl), [], ["trash"])
-    do("g", lambda e: e.iota(T.vrow[:, 0:B * (r + 1)], [[1, B * (r + 1)]], 0, 0, **fl), [], ["vrowa"])
+    do("g", lambda e: e.iota(T.jc[:, :], [[0, R], [16, TC]], 0, 0, **fl), [], ["jc"])
+    do("g", lambda e: e.iota(T.spf[:, :], [[RW, 2], [2, LC]], TC, 0, **fl), [], ["spf"])
+    do("g", lambda e: e.iota(T.row[:, :], [[1, 16], [16, RW]], 0, 0, **fl), [], ["row"])
+    do("g", lambda e: e.iota(T.vrow[:, 0:B * (r + 1)], [[1, B * (r + 1)]], K, 0, **fl), [], ["vrowa"])
     W["vrowb"] = []
     if r < N - 1:
-        do("g", lambda e: e.iota(T.vrow[:, B * (r + 1):NB], [[1, NB - B * (r + 1)]], B * r, 0, **fl), [], ["vrowb"])
+        do("g", lambda e: e.iota(T.vrow[:, B * (r + 1):NB], [[1, NB - B * (r + 1)]], K + B * r, 0, **fl), [], ["vrowb"])
     do("v", lambda e: e.memset(T.zeros[:, :], 0), [], ["zeros"])
-    for i in range(R):
-        do("v", lambda e: e.memset(T.inv[:, WIN * i:WIN * i + K], 0.0), [], ["inv%d" % i])
-    col = T.p16f[:, 0:1]
-    do("v", lambda e: e.tensor_scalar(T.p16[:, 0:1], T.pp[:, 0:1], 15, None, A.bitwise_and), ["pp"], ["p16"])
-    do("v", lambda e: e.tensor_copy(T.p16f[:, 0:1], T.p16[:, 0:1]), ["p16"], ["p16f"])
-    do("v", lambda e: e.tensor_scalar(T.mask[:, :], T.run[:, :], col, None, A.is_equal), ["run", "p16f"], ["mask"])
-    do("v", lambda e: e.tensor_scalar(T.jl[:, :], T.jc[:, :], col, None, A.add), ["jc", "p16f"], ["jl"])
-    do("v", lambda e: e.tensor_scalar(T.trash2[:, :], T.trash[:, :], col, None, A.add), ["trash", "p16f"], ["trash2"])
-    do("v", lambda e: e.tensor_copy(T.lists[:, AL:AL + TC], T.jl[:, :]), ["jl"], ["listb"])
+    do("v", lambda e: e.memset(T.ut[:, 8:512], 0.0), [], ["u0"])
+    ts(T.p16[:, 0:1], T.pp[:, 0:1], 15, A.bitwise_and, ["pp"], ["p16"])
+    ts(T.pg[:, 0:1], T.pp[:, 0:1], 4, A.arith_shift_right, ["pp"], ["pg"])
+    ts(T.pq[:, 0:1], T.pp[:, 0:1], 7, A.bitwise_and, ["pp"], ["p8"])
+    ts(T.pq[:, 2:3], T.pp[:, 0:1], 3, A.arith_shift_right, ["pp"], ["ph"], 1, A.bitwise_and)
+    p16, two, low, high, grp = (T.colf[:, i:i + 1] for i in range(5))
+    cp(p16, T.p16[:, 0:1], ["p16"], ["p16f"])
+    ts(two, T.p16[:, 0:1], 2.0, A.mult, ["p16"], ["two"])
+    ts(low, T.pq[:, 0:1], float(2 * RW), A.mult, ["p8"], ["low"])
+    cp(high, T.pq[:, 2:3], ["ph"], ["high"])
+    ts(grp, T.pg[:, 0:1], 1.0, A.add, ["pg"], ["grp"], float(LC), A.mult)
+    ts(T.both[:, 0:2 * R * TC:2], T.jc[:, :], p16, A.add, ["jc", "p16f"], ["botha"])
+    e0, e1, e2, e3, e4 = (T.ent[:, LC * i:LC * i + LC] for i in range(5))
+    ts(e0, T.jc[:, 0:LC], p16, A.add, ["jc", "p16f"], ["e0"], float(-B * r), A.add)
+    ts(e4, T.jc[:, 0:LC], p16, A.add, ["jc", "p16f"], ["e4"], float(2 * SPAN), A.mult)
+    ts(T.nxt[:, 0:1], grp, p16, A.add, ["grp", "p16f"], ["nxt"], float(AL - 1), A.min)
+    ts(T.spu[:, :], T.spf[:, :], low, A.add, ["spf", "low", "high"], ["spu"], high, A.add)
+    ts(e1, e0, 0.0, A.is_ge, ["e0"], ["e1"])
+    ts(e2, e0, float(B), A.is_lt, ["e0"], ["e2"])
+    ts(e3, e0, float(16 * (RW - 2)), A.add, ["e0"], ["e3"])
+    tt(e1, e1, e2, A.mult, ["e1", "e2"], ["e1"])
+    tt(T.kt[:, :], e1, e3, A.mult, ["e1", "e3"], ["kt"])
 
-    def quantise(k):
-        do("v", lambda e: e.quantize_mx(T["pc%d" % k][:, 0:K], T["ps%d" % k][:, 0:K], T.xt[:, :]), ["x"], ["ownc%d" % k, "owns%d" % k])
-
-    def pick(q, nm, out, win, off, rd, wr):
+    def pick(nm, out, win, off, rd, wr):
+        o, w = T[out[0] % nm][:, out[1]:out[2]], T[win[0] % nm][:, win[1]:win[2]]
         if nm == "c":
-            do("v", lambda e: e.tensor_copy(T[out[0]][:, out[2]:out[3]].bitcast(dt.uint32), T[win[0]][:, win[2]:win[3]].bitcast(dt.uint32).indirect(off)), rd, wr)
-        elif q == "v":
-            do("v", lambda e: e.tensor_copy(T[out[1]][:, out[2]:out[3]], T[win[1]][:, win[2]:win[3]].indirect(off)), rd, wr)
+            do("v", lambda e: e.tensor_copy(o.bitcast(dt.uint32), w.bitcast(dt.uint32).indirect(off)), rd, wr)
         else:
-            do("a", lambda e: e.activation(T[out[1]][:, out[2]:out[3]], T[win[1]][:, win[2]:win[3]].indirect(off), F.Copy), rd, wr)
+            do("a", lambda e: e.activation(o, w.indirect(off), F.Copy), rd, wr)
 
     def send(t):
-        codes, scales = plans[r]
-        for nm, m, scale in (("c", codes, False), ("s", scales, True)):
+        for nm, m in zip("cs", plans[r]):
             order("g", ["snd%s%d" % (nm, t)], [])
             moves = []
             for d in sorted(m):
                 rid, pid, _ring = topo.addr(cores[d])
-                a = K + NEW * t + B * (r - (r > d))
+                a = K + B * (r - (r > d))
                 src = T["s%s%d" % (nm, t)][:, B * d:B * d + B]
-                dst = T["p%s%d" % (nm, t + 1)][:, a:a + B]
-                if not scale:
+                dst = T["l%s%d" % (nm, t)][:, a:a + B]
+                if nm == "c":
                     src, dst = src.bitcast(dt.uint8), dst.bitcast(dt.uint8)
-                moves.append(RemoteDMATransfer(dst_ids=[DstId(rid=rid, pnc=pid)], dma_engine_mask=m[d], remote_sem=T.sem["arr%s%d" % (nm, t)], src=src, dst=dst))
+                moves.append(RemoteDMATransfer(dst_ids=[DstId(rid=rid, pnc=pid)], dma_engine_mask=m[d], remote_sem=T.sem["arr%d" % t], src=src, dst=dst))
             sem = "snt%d" % t
             g.remote_dma_fused(moves, local_sem=T.sem[sem])
             total[sem] = total.get(sem, 0) + sum(ones(m[d]) for d in m)
+        W["sent%d" % t] = [(sem, None)]
 
-    def fetch(t):
+    def fetch(t, rd):
         a, b = 512 * O * t, 512 * O * (t + 1)
-        dma("s", "lw%d" % t, T.wt[:, a:b], T.w[:, a:b], ["sent%d" % max(t - 1, 0)], ["w%d" % t])
+        dma("s", "lw%d" % t, T.wt[:, a:b], T.w[:, a:b], rd, ["w%d" % t])
 
-    def carry(name, k, a, b, rd):
-        for nm in ("c", "s"):
-            o, i = T["p%s%d" % (nm, k)][:, a:b], T["p%s%d" % (nm, k - 1)][:, a:b]
-            if nm == "c":
-                o, i = o.bitcast(dt.uint8), i.bitcast(dt.uint8)
-            dma("s", "%s%d" % (name, k), o, i, rd(nm), ["%s%s%d" % (name, nm, k)])
+    def pack(t):
+        a, b = 128 * O * t, 128 * O * (t + 1)
+        do("v", lambda e: e.quantize_mx(T.wc[:, a:b], T.ws[:, a:b], T.wt[:, 4 * a:4 * b]), ["w%d" % t], ["wq%d" % t])
 
-    quantise(0)
-    do("v", lambda e: e.tensor_copy(T.csu[:, :], T.csl[:, :]), ["cs"], ["csu"])
-    for nm in ("c", "s"):
-        pick("a", nm, ("sc0", "ss0", 0, NB), ("pc0", "ps0", 0, K), T.csu[:, 0:LC], ["own%s0" % nm, "csu"], ["snd%s0" % nm])
+    fetch(0, [])
+    H = K // 2
+    for i in range(2):
+        do("v", lambda e: e.quantize_mx(T.xc[:, H * i:H * i + H], T.xs[:, H * i:H * i + H], T.xt[:, 4 * H * i:4 * H * (i + 1)]), ["x%d" % i], ["xq%d" % i])
+        if i == 0:
+            cp(T.cs0[:, :], T.csl[:, 0:LC], ["cs"], ["cs0"])
+    for nm in "cs":
+        pick(nm, ("s%s0", 0, NB), ("x%s", 0, K), T.cs0[:, :], ["xq0", "xq1", "cs0"], ["snd%s0" % nm])
     send(0)
-    fetch(0)
-    fetch(1)
     do("g", lambda e: e.partition_broadcast(T.thri[:, :], T.thr1[0:1, :], 128), ["thr1"], ["thri"])
 
-    def later(t):
-        v, s, l, a = "val%d" % t, "sum%d" % t, "lin%d" % t, WIN * t
-        n = NB * (R - 1 - t)
-        do("v", lambda e: e.tensor_scalar(T[v][:, :], T.vrow[:, :], float(K + NEW * t), None, A.add), ["vrowa", "vrowb"], [v])
-        yield
-        do("v", lambda e: e.tensor_copy(T.inv[:, a:a + WIN].indirect(T.cdo[:, LC * t:LC * t + LC]), T[v][:, :]), [v, "cdo"], ["inv%d" % t])
-        yield
-        if n:
-            do("v", lambda e: e.tensor_tensor(T[l][:, 0:n], T.inv[:, a:a + K].indirect(T.csu[:, LC * (t + 1):AL]), T.mask[:, 0:n], A.mult), ["inv%d" % t, "csu", "mask"], [l + "a"])
-        do("v", lambda e: e.tensor_tensor(T[l][:, n:n + K], T.inv[:, a:a + K], T.mask[:, 0:K], A.mult), ["inv%d" % t, "mask"], [l + "b"])
-        if n:
-            do("v", lambda e: e.tensor_tensor_scan(T[s][:, 0:n], T.seg[:, 0:n], T[l][:, 0:n], 0.0, A.mult, A.add), ["seg", l + "a"], [s + "a"])
-        do("v", lambda e: e.tensor_tensor_scan(T[s][:, n:n + K], T.seg[:, 0:K], T[l][:, n:n + K], 0.0, A.mult, A.add), ["seg", l + "b"], [s + "b"])
-        yield
+    kk = T.kp[:, 0:2 * LC]
+    tt(T.kp[:, 0:LC], T.cdg[:, :], T.kt[:, :], A.max, ["cd", "kt"], ["kpa"])
+    ts(T.kp[:, LC:LC + 16], T.csl[:, :].indirect(T.nxt[:, 0:1]), 0.0, A.max, ["cs", "nxt"], ["kpb"])
+    do("v", lambda e: e.quantize_mx(T.uc[:, :], T.us[:, :], T.ut[:, :]), ["u", "u0"], ["uq"])
+    ts(T.kb[:, :], kk, 4, A.arith_shift_right, ["kpa", "kpb"], ["kb"])
+    ts(T.k1[:, :], kk, float(RW), A.mult, ["kpa", "kpb"], ["k1"])
+    ts(T.k2[:, :], T.kb[:, :], float(1 - 16 * RW), A.mult, ["kb"], ["k2"])
+    tt(T.k3[:, :], T.k1[:, :], T.k2[:, :], A.add, ["k1", "k2"], ["k3"])
+    cp(T.po[:, :], T.k3[:, :], ["k3"], ["po"])
+    cp(T.grow[:, 0:NB], T.row[:, :].indirect(T.po[:, LC:2 * LC]), ["po", "row"], ["growa"])
+    cp(T.row[:, :].indirect(T.po[:, 0:LC]), T.vrow[:, :], ["po", "vrowa", "vrowb"], ["row"])
+    cp(T.grow[:, NB:2 * NB], T.row[:, :].indirect(T.po[:, LC:2 * LC]), ["po", "row"], ["growb"])
+    cp(T.row[:, :].indirect(T.spu[:, :]), T.grow[:, :], ["spu", "growa", "growb"], ["row"])
+    for t in range(R):
+        n = min(t, 1)
+        dma("s", "lb%d" % n, T.bl[:, RW * t:RW * t + RW], T.row[16 * t:16 * t + 8, :], ["row"] + ["sent0"] * n, ["bl%d" % n])
+    fetch(1, [])
+    for nm in "cs":
+        pick(nm, ("v%s", 0, 128), ("u%s", 0, 128), T.zeros[:, :], ["uq", "zeros"], ["v" + nm])
+    do("v", lambda e: e.quantize_mx(T.lc0[:, 0:K], T.ls0[:, 0:K], T.xt[:, :]), ["x0", "x1"], ["tabc0", "tabs0"])
+    ts(T.thrf[:, :], T.thri[:, :], 2.0, A.mult, ["thri"], ["thrf"], float(-NEW), A.add)
+    ts(T.thrg[:, :], T.thri[:, :], -2.0, A.mult, ["thri"], ["thrg"], float(NEW + SPAN // 2 + 1), A.add)
 
-    def newer(t):
-        do("v", lambda e: e.tensor_tensor(T["ncf%d" % t][:, :], T.lists[:, LC * t:LC * t + LC], T["sum%d" % (t - 1)][:, 15:16 * LC:16], A.max), ["lista", "sum%da" % (t - 1)], ["ncf%d" % t])
-        yield
-        do("v", lambda e: e.tensor_copy(T["ncu%d" % t][:, :], T["ncf%d" % t][:, :]), ["ncf%d" % t], ["ncu%d" % t])
-        yield
+    def ready(t):
+        a, n = RW * t, min(t, 1)
+        if t < R - 1:
+            ts(T.base[:, LC * t:LC * t + LC], e4, T.thrg[:, t:t + 1], A.add, ["e4", "thrg"], ["base%d" % t])
+            cp(T["nl%d" % t][:, :], T.bl[:, a + TC:a + TC + 2 * LC], ["bl%d" % n], ["nl%d" % t])
+        cp(T.both[:, 2 * TC * t + 1:2 * TC * (t + 1):2], T.bl[:, a:a + TC], ["bl%d" % n], ["bothb%d" % t])
 
-    w0, n1 = later(0), newer(1)
-    quantise(1)
-    do("v", lambda e: e.tensor_scalar(T.own1[:, :], T.cdl[:, :], 0.0, None, A.is_lt), ["cd"], ["own1"])
-    do("v", lambda e: e.quantize_mx(T.uc[:, :], T.us[:, :], T.ut[:, :]), ["u"], ["uc", "us"])
-    do("v", lambda e: e.tensor_tensor(T.own2[:, :], T.own1[:, :], T.trash2[:, :], A.mult), ["own1", "trash2"], ["own2"])
-    for nm in ("c", "s"):
-        pick("a", nm, ("vc", "vs", 0, 128), ("uc", "us", 0, 128), T.zeros[:, :], ["u" + nm, "zeros"], ["v" + nm])
-    do("v", lambda e: e.tensor_tensor(T.cdf[:, :], T.cdl[:, :], T.own2[:, :], A.add), ["cd", "own2"], ["cdf"])
-    for nm in ("c", "s"):
-        pick("a", nm, ("cc1", "cs_1", 0, NB), ("pc1", "ps1", 0, K), T.csu[:, LC:2 * LC], ["own%s1" % nm, "csu"], ["nc%s1" % nm])
-    do("v", lambda e: e.tensor_copy(T.cdo[:, :], T.cdf[:, :]), ["cdf"], ["cdo"])
-    next(w0)
-    do("v", lambda e: e.tensor_scalar(T.lists[:, 0:AL], T.csl[:, :], 0.0, None, A.max), ["cs"], ["lista"])
-    next(w0)
-    do("v", lambda e: e.tensor_scalar(T.seg[:, :], T.run[:, :], 0.5, None, A.is_gt), ["run"], ["seg"])
-    next(w0)
-    next(n1)
-    do("v", lambda e: e.tensor_scalar(T.thrf[:, :], T.thri[:, :], 2.0, float(-NEW), A.mult, A.add), ["thri"], ["thrf"])
-    next(n1)
+    ready(0)
 
     for t in range(R):
-        k = n = t + 1
-        end = K + NEW * k
-        num, bit = T["num%d" % t], T["bit%d" % t]
-        past = lambda x, j: (["cp%s%d" % (x, j)] if j > 1 else []) + (["co%s%d" % (x, j)] if j > 2 else [])
-        held = lambda x: ["own%s%d" % (x, k), "land%s%d" % (x, t)] + past(x, k)
-        if t < R - 1:
-            carry("cp", k + 1, end - NEW, end, lambda x: ["land%s%d" % (x, t)])
+        n = t + 1
+        held = lambda x: ["tab%s%d" % (x, t), "land%d" % t]
+        win = ("l%%s%d" % t, 0, END)
         sb = 512 * (t % 2)
-        do("p", lambda e: e.matmul_mx(T.acc[:, sb:sb + 128], T.vc[:, :], T.vs[:, :], T["pc%d" % k][:, end - 128:end], T["ps%d" % k][:, end - 128:end], True, True), ["vc", "vs"] + held("c") + held("s"), ["acc%d" % (t % 2)])
+        cnt = T["num%d" % t][:, 0:1]
+        do("p", lambda e: e.matmul_mx(T.acc[:, sb:sb + 128], T.vc[:, :], T.vs[:, :], T["lc%d" % t][:, END - 128:END], T["ls%d" % t][:, END - 128:END], True, True), ["vc", "vs"] + held("c") + held("s"), ["acc%d" % (t % 2)])
+        sign = lambda: do("a", lambda e: e.activation(T["bit%d" % t][:, :], T.acc[:, sb + 128 - NEW:sb + 128], F.Sign, bias=TINY, accum_out=cnt), ["acc%d" % (t % 2)], ["cnt%d" % t])
         if t < R - 1:
-            out, off, cv = ("cc%d" % n, "cs_%d" % n, STEP, STEP + NB), T["ncu%d" % n][:, :], "ncu%d" % n
-        else:
-            out, off, cv = ("ttc", "tts", K, 2 * K), T.fcu[:, :], "fcu"
-        win = ("pc%d" % k, "ps%d" % k, 0, end)
-        for nm in ("c", "s"):
-            pick("v", nm, out, win, off, held(nm) + [cv], ["wc%s%d" % (nm, n)])
-        do("a", lambda e: e.activation(bit[:, :], T.acc[:, sb + 128 - NEW:sb + 128], F.Sign, bias=TINY, accum_out=num[:, 0:1]), ["acc%d" % (t % 2)], ["cnt%d" % t])
-        step, width = (STEP, LC) if t < R - 1 else (K, TC)
-        do("v", lambda e: e.tensor_scalar(num[:, 4:5], num[:, 0:1], T.thrf[:, t:t + 1], float(step), A.is_ge, A.mult), ["cnt%d" % t, "thrf"], ["shift%d" % t])
-        pkl = T["pk%d" % n] if t < R - 1 else T.pkl
-        do("v", lambda e: e.tensor_scalar(pkl[:, :], T.jl[:, 0:width], num[:, 4:5], None, A.add), ["jl", "shift%d" % t], ["pk%d" % n])
-        if t < R - 1:
-            src, dst = ("cc%d" % n, "cs_%d" % n, 0, STEP + NB), ("sc%d" % n, "ss%d" % n, 0, NB)
-            for nm in ("c", "s"):
-                pick("a", nm, dst, src, pkl[:, :], ["nc%s%d" % (nm, n), "wc%s%d" % (nm, n), "pk%d" % n], ["snd%s%d" % (nm, n)])
+            both = {"c": "cc%d" % t, "s": "cs%dx" % t}
+            for h, nm in ((0, "c"), (0, "s"), (1, "c"), (1, "s")):
+                if (h, nm) == (1, "s"):
+                    sign()
+                pick(nm, (both[nm] + "%.0s", NB * h, NB * h + NB), win, T["nl%d" % t][:, LC * h:LC * h + LC], held(nm) + ["nl%d" % t], ["c%s%d%d" % (nm, t, h)])
+            ts(T["pk%d" % t][:, :], T.base[:, LC * t:LC * t + LC], cnt, A.add, ["base%d" % t, "cnt%d" % t], ["pk%d" % t], 1.0 / SPAN, A.mult)
+            for nm in "cs":
+                pick(nm, ("s%%s%d" % n, 0, NB), (both[nm] + "%.0s", 0, 2 * NB), T["pk%d" % t][:, :], ["c%s%d0" % (nm, t), "c%s%d1" % (nm, t), "pk%d" % t], ["snd%s%d" % (nm, n)])
             send(n)
-            wn = later(n)
-            lo = LC * (t + 2)
-            wid = AL + TC - lo
-            tmp, lu, sm = T["tmp%d" % t], T["lu%d" % t], T["sum%d" % t]
-            do("v", lambda e: e.tensor_scalar(tmp[:, 0:wid], sm[:, 16 * LC + 15:16 * (LC + wid):16], num[:, 4:5], 1.0 / STEP, A.mult, A.mult), ["sum%da" % t, "sum%db" % t, "shift%d" % t], ["tmp%d" % t])
-            next(wn)
-            do("v", lambda e: e.tensor_tensor(T.lists[:, lo:AL + TC], T.lists[:, lo:AL + TC], tmp[:, 0:wid], A.max), ["tmp%d" % t, "lista", "listb"], ["lista", "listb"])
-            next(wn)
-            do("v", lambda e: e.tensor_copy(lu[:, lo:AL + TC], T.lists[:, lo:AL + TC]), ["lista", "listb"], ["lu%d" % t])
-            for i in [t] + ([n] if t == R - 2 else []):
-                a, b = 128 * O * i, 128 * O * (i + 1)
-                do("v", lambda e: e.quantize_mx(T.wc[:, a:b], T.ws[:, a:b], T.wt[:, 4 * a:4 * b]), ["w%d" % i], ["wq%d" % i])
-            tab = ("tc%d" % t, "ts%d" % t, 0, K) if t < R - 2 else ("ttc", "tts", 0, K)
-            for nm in ("c", "s"):
-                pick("a", nm, tab, win, lu[:, AL:AL + TC], held(nm) + ["lu%d" % t], ["tab%s%d" % (nm, t)])
-            for o in range(O):
-                i = O * t + o
-                pb = 512 * (i % 4)
-                do("p", lambda e: e.matmul_mx(T.prod[:, pb:pb + K], T.wc[:, 128 * i:128 * i + 128], T.ws[:, 128 * i:128 * i + 128], T[tab[0]][:, 0:K], T[tab[1]][:, 0:K], True, True), ["wq%d" % t, "tabc%d" % t, "tabs%d" % t], ["prod%d" % (i % 4)])
-            for o in range(O):
-                i = O * t + o
-                pb = 512 * (i % 4)
-                do("a", lambda e: e.activation(T.ty[:, K * i:K * i + K], T.prod[:, pb:pb + K], F.Copy), ["prod%d" % (i % 4)], ["ty%d" % i])
-            if n + 1 < R:
-                fetch(n + 1)
-            if k + 2 <= R:
-                carry("co", k + 2, K, end, lambda x: ["sent%d" % n] + past(x, k + 1))
-            y = slice(O * K * t, O * K * (t + 1))
-            dma("s", "yo%d" % t, T.y[:, y], T.ty[:, y], ["sent%d" % n, "ty%d" % (O * t), "ty%d" % (O * t + 1)], ["out%d" % t])
-            next(wn)
-            quantise(k + 1)
-            if t < R - 2:
-                m = n + 1
-                nw = newer(m)
-                next(nw)
-                src = ("pc%d" % (k + 1), "ps%d" % (k + 1), 0, end)
-                for nm in ("c", "s"):
-                    pick("a", nm, ("cc%d" % m, "cs_%d" % m, 0, NB), src, lu[:, LC * m:LC * m + LC], ["own%s%d" % (nm, k + 1), "lu%d" % t] + past(nm, k + 1), ["nc%s%d" % (nm, m)])
-                next(nw)
-            else:
-                do("v", lambda e: e.tensor_tensor(T.fcf[:, :], T.lists[:, AL:AL + TC], T["sum%d" % n][:, 15:16 * TC:16], A.max), ["listb", "sum%db" % n], ["fcf"])
-                do("v", lambda e: e.tensor_copy(T.fcu[:, :], T.fcf[:, :]), ["fcf"], ["fcu"])
         else:
-            H = K // 2
+            sign()
+            for q in "va":
+                order(q, ["land%d" % t], [])
+        sel, tl = T["sel%d" % t][:, 0:1], T["tl%d" % t]
+        ts(sel, cnt, T.thrf[:, t:t + 1], A.is_ge, ["cnt%d" % t, "thrf", "two"], ["sel%d" % t], two, A.add)
+        cp(tl[:, :], T.both[:, 2 * TC * t:2 * TC * (t + 1)].indirect(sel), ["sel%d" % t, "botha", "bothb%d" % t], ["tl%d" % t])
+        if t < R - 1:
+            for nm in "cs":
+                pick(nm, ("l%%s%d" % n, 0, K), win, tl[:, :], held(nm) + ["tl%d" % t], ["tab%s%d" % (nm, n)])
+            pack(t)
+            ready(n)
+            if t == R - 2:
+                pack(n)
+            for o in range(O):
+                i = O * t + o
+                pb = 512 * (i % 4)
+                do("p", lambda e: e.matmul_mx(T.prod[:, pb:pb + K], T.wc[:, 128 * i:128 * i + 128], T.ws[:, 128 * i:128 * i + 128], T["lc%d" % n][:, 0:K], T["ls%d" % n][:, 0:K], True, True), ["wq%d" % t, "tabc%d" % n, "tabs%d" % n], ["prod%d" % (i % 4)])
+            for o in range(O):
+                i = O * t + o
+                pb = 512 * (i % 4)
+                if o:
+                    do("a", lambda e: e.activation(T.ty[:, K * i:K * i + K], T.prod[:, pb:pb + K], F.Copy), ["prod%d" % (i % 4)], ["ty%d" % i])
+                else:
+                    cp(T.ty[:, K * i:K * i + K], T.prod[:, pb:pb + K], ["prod%d" % (i % 4)], ["ty%d" % i])
+            y = slice(O * K * t, O * K * (t + 1))
+            dma("s", "yo%d" % t, T.y[:, y], T.ty[:, y], ["ty%d" % (O * t), "ty%d" % (O * t + 1)], ["out%d" % t])
+            if n + 1 < R:
+                fetch(n + 1, [])
+        else:
             for h in range(2):
-                tab = ("tc%d" % t, "ts%d" % t, H * h, H * h + H)
-                for nm in ("c", "s"):
-                    pick("a", nm, tab, ("ttc", "tts", 0, 2 * K), pkl[:, TC // 2 * h:TC // 2 * (h + 1)], ["tab%s%d" % (nm, t - 1), "wc%s%d" % (nm, n), "pk%d" % n], ["tab%s%d%d" % (nm, t, h)])
+                for nm in "cs":
+                    pick(nm, ("l%%s%d" % n, H * h, H * h + H), win, tl[:, TC // 2 * h:TC // 2 * (h + 1)], held(nm) + ["tl%d" % t], ["tab%s%d%d" % (nm, n, h)])
                 for o in range(O):
                     i = O * t + o
                     pb = 512 * (2 * h + o)
-                    do("p", lambda e: e.matmul_mx(T.prod[:, pb:pb + H], T.wc[:, 128 * i:128 * i + 128], T.ws[:, 128 * i:128 * i + 128], T[tab[0]][:, tab[2]:tab[3]], T[tab[1]][:, tab[2]:tab[3]], True, True), ["wq%d" % t, "tabc%d%d" % (t, h), "tabs%d%d" % (t, h)], ["prod%d" % (2 * h + o)])
+                    do("p", lambda e: e.matmul_mx(T.prod[:, pb:pb + H], T.wc[:, 128 * i:128 * i + 128], T.ws[:, 128 * i:128 * i + 128], T["lc%d" % n][:, H * h:H * h + H], T["ls%d" % n][:, H * h:H * h + H], True, True), ["wq%d" % t, "tabc%d%d" % (n, h), "tabs%d%d" % (n, h)], ["prod%d" % (2 * h + o)])
             for h in range(2):
                 for o in range(O):
                     a, pb = K * (O * t + o) + H * h, 512 * (2 * h + o)
@@ -376,7 +342,7 @@ def rank_program(g, core, T, topo):
                     if o:
                         do("a", lambda e: e.activation(T.ty[:, y], T.prod[:, pb:pb + H], F.Copy), ["prod%d" % (2 * h + o)], ["tyz%d%d" % (h, o)])
                     else:
-                        do("v", lambda e: e.tensor_copy(T.ty[:, y], T.prod[:, pb:pb + H]), ["prod%d" % (2 * h + o)], ["tyz%d%d" % (h, o)])
+                        cp(T.ty[:, y], T.prod[:, pb:pb + H], ["prod%d" % (2 * h + o)], ["tyz%d%d" % (h, o)])
                     q, sem = ("a", "yp") if o and h else ("s", "yo%d" % t)
                     dma(q, sem, T.y[:, y], T.ty[:, y], ["tyz%d%d" % (h, o)], ["outz%d%d" % (h, o)])
 

@@ -8,8 +8,8 @@ END = K + NEW
 LC = NB // 16
 TC = K // 16
 AL = R * LC
-RW = TC + 2 * LC + 2
-SPAN = 256
+WIN = K + 16
+SPAN = 512
 TINY = 1e-30
 
 CODE, BYTE = "float8_e4m3fn_x4", "uint8"
@@ -18,23 +18,21 @@ SCRATCH = {
     "xt": ("sbuf", [128, 4 * K], "bfloat16"),
     "ut": ("sbuf", [128, 512], "bfloat16"),
     "wt": ("sbuf", [128, 512 * R * O], "bfloat16"),
-    "csl": ("sbuf", [128, AL], I32), "cdg": ("sbuf", [128, LC], I32),
+    "csl": ("sbuf", [128, LC], I32), "cdg": ("sbuf", [128, LC], I32), "csg": ("sbuf", [128, LC], I32),
+    "last": ("sbuf", [128, 5 * TC + 2], F32),
     "cs0": ("sbuf", [128, LC], U16),
     "thr1": ("sbuf", [1, 16], I32), "thri": ("sbuf", [128, 16], I32), "thrf": ("sbuf", [128, 16], F32),
-    "pp": ("sbuf", [128, 2], I32), "p16": ("sbuf", [128, 2], I32), "pg": ("sbuf", [128, 2], I32),
-    "pq": ("sbuf", [128, 4], I32),
+    "pp": ("sbuf", [128, 2], I32), "p16": ("sbuf", [128, 2], I32),
     "colf": ("sbuf", [128, 8], F32),
-    "nxt": ("sbuf", [128, 2], U16),
     "jc": ("sbuf", [128, R * TC], F32),
-    "ent": ("sbuf", [128, 5 * LC], F32), "kt": ("sbuf", [128, LC], F32),
+    "ent": ("sbuf", [128, LC], F32),
     "thrg": ("sbuf", [128, 16], F32), "base": ("sbuf", [128, R * LC], F32),
-    "spf": ("sbuf", [128, 2 * LC], F32), "spu": ("sbuf", [128, 2 * LC], U16),
-    "kp": ("sbuf", [128, LC + 16], I32), "kb": ("sbuf", [128, 2 * LC], I32),
-    "k1": ("sbuf", [128, 2 * LC], F32), "k2": ("sbuf", [128, 2 * LC], F32), "k3": ("sbuf", [128, 2 * LC], F32),
-    "po": ("sbuf", [128, 2 * LC], U16),
-    "vrow": ("sbuf", [128, NB], F32), "grow": ("sbuf", [128, 2 * NB], F32),
-    "row": ("sbuf", [128, 16 * RW], F32),
-    "bl": ("sbuf", [128, R * RW], F32),
+    "pat": ("sbuf", [128, 32], F32), "turn": ("sbuf", [128, 32], U16),
+    "cdo": ("sbuf", [128, LC], U16), "cso": ("sbuf", [128, LC], U16),
+    "vrow": ("sbuf", [128, NB], F32), "grow": ("sbuf", [128, 2 * NB + 32], F32),
+    "row": ("sbuf", [128, WIN], F32), "keys": ("sbuf", [128, K], F32),
+    "trow": ("sbuf", [128, K], F32), "srow": ("sbuf", [128, 256], U16),
+    "bl": ("sbuf", [128, R * TC], F32), "nl": ("sbuf", [128, 16 * R], U16),
     "both": ("sbuf", [128, 2 * R * TC], F32),
     "zeros": ("sbuf", [128, 8], U16),
     "uc": ("sbuf", [128, 128], CODE), "us": ("sbuf", [128, 128], BYTE),
@@ -55,37 +53,33 @@ for _t in range(R):
     SCRATCH["num%d" % _t] = ("sbuf", [128, 2], F32)
     SCRATCH["sel%d" % _t] = ("sbuf", [128, 2], U16)
     SCRATCH["tl%d" % _t] = ("sbuf", [128, TC], U16)
-    if _t < R - 1:
-        SCRATCH["nl%d" % _t] = ("sbuf", [128, 2 * LC], U16)
-        SCRATCH["pk%d" % _t] = ("sbuf", [128, LC], U16)
-        SCRATCH["cc%d" % _t] = ("sbuf", [128, 2 * NB], CODE)
-        SCRATCH["cs%dx" % _t] = ("sbuf", [128, 2 * NB], BYTE)
+    SCRATCH["pk%d" % _t] = ("sbuf", [128, LC], U16)
+    SCRATCH["bc%d" % _t] = ("sbuf", [128, 2 * NB + (K if _t == R - 1 else 0)], CODE)
+    SCRATCH["bs%d" % _t] = ("sbuf", [128, 2 * NB + (K if _t == R - 1 else 0)], BYTE)
 
-SEMAPHORES = ["vq", "aq", "pq", "gq", "lx0", "lx1", "lcs", "lcd", "lu", "lt", "yp", "lb0", "lb1"]
+SEMAPHORES = ["vq", "aq", "pq", "gq", "lx0", "lx1", "lcs", "lcd", "lu", "lt", "yp", "lb0", "lb1", "ln0", "ln1", "lcn"]
 for _t in range(R):
     SEMAPHORES += ["snt%d" % _t, "arr%d" % _t, "yo%d" % _t, "lw%d" % _t]
 
 
 def deal(topo, cores, s):
     src = cores[s]
-    home, off = [], []
-    for d in range(len(cores)):
-        if d != s:
-            (home if topo.chip(cores[d]) == topo.chip(src) else off).append(d)
-    near = lambda d: topo.mates(topo.chip(src), topo.chip(cores[d])) or topo.same_plane(topo.chip(src), topo.chip(cores[d]))
-    eng = topo.engines(src, cores[off[0]])
-    even, odd = eng[0::2], eng[1::2]
-    two = len(eng) - len(off)
-    off = [d for d in off if not near(d)] + [d for d in off if near(d)]
-    codes, scales = {}, {}
-    for i, d in enumerate(off):
-        codes[d] = even[2 * i:2 * i + 2] if i < two else [odd[i - two]]
-        scales[d] = odd[2 * i:2 * i + 2] if i < two else [even[i - two]]
-    for d in home:
-        rest = [e for e in topo.engines(src, cores[d]) if e not in eng]
-        codes[d] = scales[d] = rest[::max(1, len(rest) // 2)][:2]
-    bits = lambda m: {d: sum(1 << e for e in m[d]) for d in m}
-    return bits(codes), bits(scales)
+    here = topo.chip(src)
+    way = lambda c: 2 if topo.mates(here, c) else 1 if topo.same_plane(here, c) else 0
+    chips = sorted({topo.chip(c) for c in cores} - {here}, key=way)
+    on = lambda c: [d for d in range(len(cores)) if d != s and topo.chip(cores[d]) == c]
+    bits = lambda es: sum(1 << e for e in es)
+    calls = []
+    for c in chips:
+        ds = on(c)
+        eng = topo.engines(src, cores[ds[0]])
+        for h, nm in enumerate("cs"):
+            m = {d: bits(eng[i::len(ds)]) for i, d in enumerate(ds)}
+            if c == chips[-1]:
+                for d in on(here):
+                    m[d] = bits([e for e in topo.engines(src, cores[d]) if e not in eng][2 * h::4])
+            calls.append((nm, m))
+    return calls
 
 
 def rank_program(g, core, T, topo):
@@ -158,52 +152,55 @@ def rank_program(g, core, T, topo):
         do("v", lambda e: e.tensor_copy(out, in_), rd, wr)
 
     for t in range(R):
-        total["arr%d" % t] = sum(ones(plans[s][h][r]) for s in range(N) if s != r for h in range(2))
+        total["arr%d" % t] = sum(ones(m.get(r, 0)) for plan in plans for _nm, m in plan)
         W["land%d" % t] = [("arr%d" % t, None)]
 
     h = 2 * K
     dma("s", "lx0", T.xt[:, 0:h], T.x[:, 0:h], [], ["x0"])
-    dma("s", "lx1", T.xt[:, h:2 * h], T.x[:, h:2 * h], [], ["x1"])
     for i in range(8):
-        dma("a" if i < 5 else "s", "lcs", T.csl[16 * i:16 * i + 16, :], T.cs[:, :], [], ["cs"])
+        dma("a" if i < 5 else "s", "lcs", T.csl[16 * i:16 * i + 16, :], T.cs[:, 0:LC], [], ["cs"])
     dma("a", "lt", T.thr1[0:1, :], T.thr[:, :], [], ["thr1"])
+    dma("s", "lx1", T.xt[:, h:2 * h], T.x[:, h:2 * h], [], ["x1"])
     for i in range(8):
         t = min(i, R - 1)
         dma("sa"[i % 2], "lcd", T.cdg[16 * i:16 * i + 16, :], T.cd[:, LC * t:LC * t + LC], [], ["cd"])
+    for i in range(8):
+        src = T.cs[:, LC * (i + 1):LC * (i + 2)] if i < R - 1 else T.cd[:, LC * (R - 1):LC * R]
+        dma("sa"[i % 2], "lcn", T.csg[16 * i:16 * i + 16, :], src, [], ["csg"])
     dma("s", "lu", T.ut[:, 0:8], T.u[:, 0:8], [], ["u"])
 
     fl = {"allow_small_or_imprecise_dtypes": True}
     do("g", lambda e: e.iota(T.pp[:, 0:1], [[0, 1]], 0, 1), [], ["pp"])
     do("g", lambda e: e.iota(T.jc[:, :], [[0, R], [16, TC]], 0, 0, **fl), [], ["jc"])
-    do("g", lambda e: e.iota(T.spf[:, :], [[RW, 2], [2, LC]], TC, 0, **fl), [], ["spf"])
-    do("g", lambda e: e.iota(T.row[:, :], [[1, 16], [16, RW]], 0, 0, **fl), [], ["row"])
+    do("g", lambda e: e.iota(T.pat[:, 0:16], [[1, 8], [NB, 2]], 0, 0, **fl), [], ["pata"])
+    do("g", lambda e: e.iota(T.pat[:, 16:32], [[1, 16]], 0, 0, **fl), [], ["patb"])
+    do("g", lambda e: e.iota(T.row[:, :], [[1, WIN]], 0, 0, **fl), [], ["row"])
     do("g", lambda e: e.iota(T.vrow[:, 0:B * (r + 1)], [[1, B * (r + 1)]], K, 0, **fl), [], ["vrowa"])
     W["vrowb"] = []
     if r < N - 1:
         do("g", lambda e: e.iota(T.vrow[:, B * (r + 1):NB], [[1, NB - B * (r + 1)]], K + B * r, 0, **fl), [], ["vrowb"])
     do("v", lambda e: e.memset(T.zeros[:, :], 0), [], ["zeros"])
     do("v", lambda e: e.memset(T.ut[:, 8:512], 0.0), [], ["u0"])
-    ts(T.p16[:, 0:1], T.pp[:, 0:1], 15, A.bitwise_and, ["pp"], ["p16"])
-    ts(T.pg[:, 0:1], T.pp[:, 0:1], 4, A.arith_shift_right, ["pp"], ["pg"])
-    ts(T.pq[:, 0:1], T.pp[:, 0:1], 7, A.bitwise_and, ["pp"], ["p8"])
-    ts(T.pq[:, 2:3], T.pp[:, 0:1], 3, A.arith_shift_right, ["pp"], ["ph"], 1, A.bitwise_and)
-    p16, two, low, high, grp = (T.colf[:, i:i + 1] for i in range(5))
-    cp(p16, T.p16[:, 0:1], ["p16"], ["p16f"])
-    ts(two, T.p16[:, 0:1], 2.0, A.mult, ["p16"], ["two"])
-    ts(low, T.pq[:, 0:1], float(2 * RW), A.mult, ["p8"], ["low"])
-    cp(high, T.pq[:, 2:3], ["ph"], ["high"])
-    ts(grp, T.pg[:, 0:1], 1.0, A.add, ["pg"], ["grp"], float(LC), A.mult)
+    do("v", lambda e: e.memset(T.grow[:, 2 * NB:], 0.0), [], ["growc"])
+    pi = T.p16[:, 0:1]
+    ts(pi, T.pp[:, 0:1], 15, A.bitwise_and, ["pp"], ["p16"])
+    p16, two, p8x, p16x, cap = (T.colf[:, i:i + 1] for i in range(5))
+    cp(p16, pi, ["p16"], ["p16f"])
+    ts(two, pi, 2.0, A.mult, ["p16"], ["two"])
+    ts(p8x, pi, 8.0, A.mult, ["p16"], ["p8x"])
+    ts(p16x, pi, 16.0, A.mult, ["p16"], ["p16x"])
+    ts(cap, pi, float(K), A.add, ["p16"], ["cap"])
+    own = {}
+    for c in range(LC):
+        lo, hi = max(B * r - 16 * c, 0), min(B * r + B - 16 * c, 16)
+        if lo < hi:
+            own[c] = T.colf[:, 6 + len(own):7 + len(own)]
+            ts(own[c], pi, 0.5 - (lo or hi), A.add, ["p16"], ["own%d" % c], 4.0 * K * (1 if lo else -1), A.mult)
+    ts(T.turn[:, 0:16], T.pat[:, 0:16], p8x, A.add, ["pata", "p8x"], ["turna"])
+    ts(T.turn[:, 16:32], T.pat[:, 16:32], p16x, A.add, ["patb", "p16x"], ["turnb"])
     ts(T.both[:, 0:2 * R * TC:2], T.jc[:, :], p16, A.add, ["jc", "p16f"], ["botha"])
-    e0, e1, e2, e3, e4 = (T.ent[:, LC * i:LC * i + LC] for i in range(5))
-    ts(e0, T.jc[:, 0:LC], p16, A.add, ["jc", "p16f"], ["e0"], float(-B * r), A.add)
-    ts(e4, T.jc[:, 0:LC], p16, A.add, ["jc", "p16f"], ["e4"], float(2 * SPAN), A.mult)
-    ts(T.nxt[:, 0:1], grp, p16, A.add, ["grp", "p16f"], ["nxt"], float(AL - 1), A.min)
-    ts(T.spu[:, :], T.spf[:, :], low, A.add, ["spf", "low", "high"], ["spu"], high, A.add)
-    ts(e1, e0, 0.0, A.is_ge, ["e0"], ["e1"])
-    ts(e2, e0, float(B), A.is_lt, ["e0"], ["e2"])
-    ts(e3, e0, float(16 * (RW - 2)), A.add, ["e0"], ["e3"])
-    tt(e1, e1, e2, A.mult, ["e1", "e2"], ["e1"])
-    tt(T.kt[:, :], e1, e3, A.mult, ["e1", "e3"], ["kt"])
+    ts(T.ent[:, :], T.jc[:, 0:LC], p16, A.add, ["jc", "p16f"], ["ent"], float(2 * SPAN), A.mult)
+    do("a", lambda e: e.activation(T.keys[:, :], T.row[:, 0:K], F.Copy), ["row"], ["keys"])
 
     def pick(nm, out, win, off, rd, wr):
         o, w = T[out[0] % nm][:, out[1]:out[2]], T[win[0] % nm][:, win[1]:win[2]]
@@ -213,7 +210,7 @@ def rank_program(g, core, T, topo):
             do("a", lambda e: e.activation(o, w.indirect(off), F.Copy), rd, wr)
 
     def send(t):
-        for nm, m in zip("cs", plans[r]):
+        for nm, m in plans[r]:
             order("g", ["snd%s%d" % (nm, t)], [])
             moves = []
             for d in sorted(m):
@@ -238,6 +235,8 @@ def rank_program(g, core, T, topo):
         do("v", lambda e: e.quantize_mx(T.wc[:, a:b], T.ws[:, a:b], T.wt[:, 4 * a:4 * b]), ["w%d" % t], ["wq%d" % t])
 
     fetch(0, [])
+    fetch(1, [])
+    do("g", lambda e: e.partition_broadcast(T.thri[:, :], T.thr1[0:1, :], 128), ["thr1"], ["thri"])
     H = K // 2
     for i in range(2):
         do("v", lambda e: e.quantize_mx(T.xc[:, H * i:H * i + H], T.xs[:, H * i:H * i + H], T.xt[:, 4 * H * i:4 * H * (i + 1)]), ["x%d" % i], ["xq%d" % i])
@@ -246,39 +245,39 @@ def rank_program(g, core, T, topo):
     for nm in "cs":
         pick(nm, ("s%s0", 0, NB), ("x%s", 0, K), T.cs0[:, :], ["xq0", "xq1", "cs0"], ["snd%s0" % nm])
     send(0)
-    do("g", lambda e: e.partition_broadcast(T.thri[:, :], T.thr1[0:1, :], 128), ["thr1"], ["thri"])
 
-    kk = T.kp[:, 0:2 * LC]
-    tt(T.kp[:, 0:LC], T.cdg[:, :], T.kt[:, :], A.max, ["cd", "kt"], ["kpa"])
-    ts(T.kp[:, LC:LC + 16], T.csl[:, :].indirect(T.nxt[:, 0:1]), 0.0, A.max, ["cs", "nxt"], ["kpb"])
+    here = []
+    for c in range(LC):
+        if c in own:
+            ts(T.cdo[:, c:c + 1], T.cdg[:, c:c + 1], own[c], A.max, ["cd", "own%d" % c, "cap"], ["cdo%d" % c], cap, A.min)
+            here.append("cdo%d" % c)
+    for a, b in ((0, min(own)), (max(own) + 1, LC)):
+        if a < b:
+            cp(T.cdo[:, a:b], T.cdg[:, a:b], ["cd"], ["cdo%d" % a])
+            here.append("cdo%d" % a)
+    cp(T.cso[:, :], T.csg[:, :], ["csg"], ["cso"])
     do("v", lambda e: e.quantize_mx(T.uc[:, :], T.us[:, :], T.ut[:, :]), ["u", "u0"], ["uq"])
-    ts(T.kb[:, :], kk, 4, A.arith_shift_right, ["kpa", "kpb"], ["kb"])
-    ts(T.k1[:, :], kk, float(RW), A.mult, ["kpa", "kpb"], ["k1"])
-    ts(T.k2[:, :], T.kb[:, :], float(1 - 16 * RW), A.mult, ["kb"], ["k2"])
-    tt(T.k3[:, :], T.k1[:, :], T.k2[:, :], A.add, ["k1", "k2"], ["k3"])
-    cp(T.po[:, :], T.k3[:, :], ["k3"], ["po"])
-    cp(T.grow[:, 0:NB], T.row[:, :].indirect(T.po[:, LC:2 * LC]), ["po", "row"], ["growa"])
-    cp(T.row[:, :].indirect(T.po[:, 0:LC]), T.vrow[:, :], ["po", "vrowa", "vrowb"], ["row"])
-    cp(T.grow[:, NB:2 * NB], T.row[:, :].indirect(T.po[:, LC:2 * LC]), ["po", "row"], ["growb"])
-    cp(T.row[:, :].indirect(T.spu[:, :]), T.grow[:, :], ["spu", "growa", "growb"], ["row"])
+    cp(T.row[:, :].indirect(T.cdo[:, :]), T.vrow[:, :], here + ["vrowa", "vrowb"], ["row"])
+    do("a", lambda e: e.activation(T.grow[:, 0:NB], T.keys[:, :].indirect(T.cso[:, 0:LC]), F.Copy), ["keys", "cso"], ["growa"])
+    pick("c", ("v%s", 0, 128), ("u%s", 0, 128), T.zeros[:, :], ["uq", "zeros"], ["vc"])
+    cp(T.grow[:, NB:2 * NB], T.row[:, :].indirect(T.cso[:, 0:LC]), ["cso", "row"], ["growb"])
+    do("a", lambda e: e.activation(T.trow[:, :], T.row[:, :].indirect(T.turn[:, 16:32]), F.Copy), ["row", "turnb"], ["trow"])
+    pick("s", ("v%s", 0, 128), ("u%s", 0, 128), T.zeros[:, :], ["uq", "zeros"], ["vs"])
+    do("v", lambda e: e.quantize_mx(T.lc0[:, 0:K], T.ls0[:, 0:K], T.xt[:, :]), ["x0", "x1"], ["tabc0", "tabs0"])
+    cp(T.srow[:, :], T.grow[:, :].indirect(T.turn[:, 0:16]), ["growa", "growb", "growc", "turna"], ["srow"])
     for t in range(R):
         n = min(t, 1)
-        dma("s", "lb%d" % n, T.bl[:, RW * t:RW * t + RW], T.row[16 * t:16 * t + 8, :], ["row"] + ["sent0"] * n, ["bl%d" % n])
-    fetch(1, [])
-    for nm in "cs":
-        pick(nm, ("v%s", 0, 128), ("u%s", 0, 128), T.zeros[:, :], ["uq", "zeros"], ["v" + nm])
-    do("v", lambda e: e.quantize_mx(T.lc0[:, 0:K], T.ls0[:, 0:K], T.xt[:, :]), ["x0", "x1"], ["tabc0", "tabs0"])
-    ts(T.thrf[:, :], T.thri[:, :], 2.0, A.mult, ["thri"], ["thrf"], float(-NEW), A.add)
+        if True:
+            dma("s", "ln%d" % n, T.nl[:, 16 * t:16 * t + 16], T.srow[16 * t:16 * t + 8, :], ["srow"] + ["sent0"] * n, ["nl%d" % n])
+        dma("s", "lb%d" % n, T.bl[:, TC * t:TC * t + TC], T.trow[16 * t:16 * t + 8, :], ["trow"], ["bl%d" % n])
     ts(T.thrg[:, :], T.thri[:, :], -2.0, A.mult, ["thri"], ["thrg"], float(NEW + SPAN // 2 + 1), A.add)
+    ts(T.thrf[:, :], T.thri[:, :], 2.0, A.mult, ["thri"], ["thrf"], float(-NEW), A.add)
+    for t in range(R - 1):
+        ts(T.base[:, LC * t:LC * t + LC], T.ent[:, :], T.thrg[:, t:t + 1], A.add, ["ent", "thrg"], ["base%d" % t])
+    pack(0)
 
     def ready(t):
-        a, n = RW * t, min(t, 1)
-        if t < R - 1:
-            ts(T.base[:, LC * t:LC * t + LC], e4, T.thrg[:, t:t + 1], A.add, ["e4", "thrg"], ["base%d" % t])
-            cp(T["nl%d" % t][:, :], T.bl[:, a + TC:a + TC + 2 * LC], ["bl%d" % n], ["nl%d" % t])
-        cp(T.both[:, 2 * TC * t + 1:2 * TC * (t + 1):2], T.bl[:, a:a + TC], ["bl%d" % n], ["bothb%d" % t])
-
-    ready(0)
+        cp(T.both[:, 2 * TC * t + 1:2 * TC * (t + 1):2], T.bl[:, TC * t:TC * t + TC], ["bl%d" % min(t, 1)], ["bothb%d" % t])
 
     for t in range(R):
         n = t + 1
@@ -288,30 +287,26 @@ def rank_program(g, core, T, topo):
         cnt = T["num%d" % t][:, 0:1]
         do("p", lambda e: e.matmul_mx(T.acc[:, sb:sb + 128], T.vc[:, :], T.vs[:, :], T["lc%d" % t][:, END - 128:END], T["ls%d" % t][:, END - 128:END], True, True), ["vc", "vs"] + held("c") + held("s"), ["acc%d" % (t % 2)])
         sign = lambda: do("a", lambda e: e.activation(T["bit%d" % t][:, :], T.acc[:, sb + 128 - NEW:sb + 128], F.Sign, bias=TINY, accum_out=cnt), ["acc%d" % (t % 2)], ["cnt%d" % t])
+        first, tl = (0 if t < R - 1 else K), T["tl%d" % t]
+        for h, nm in ((0, "c"), (0, "s"), (1, "c"), (1, "s")):
+            if (h, nm) == (1, "s"):
+                sign()
+            pick(nm, ("b%%s%d" % t, first + NB * h, first + NB * h + NB), win, T.nl[:, 16 * t + LC * h:16 * t + LC * h + LC], held(nm) + ["nl%d" % min(t, 1)], ["c%s%d%d" % (nm, t, h)])
+        pairs = lambda x: ["c%s%d0" % (x, t), "c%s%d1" % (x, t)]
         if t < R - 1:
-            both = {"c": "cc%d" % t, "s": "cs%dx" % t}
-            for h, nm in ((0, "c"), (0, "s"), (1, "c"), (1, "s")):
-                if (h, nm) == (1, "s"):
-                    sign()
-                pick(nm, (both[nm] + "%.0s", NB * h, NB * h + NB), win, T["nl%d" % t][:, LC * h:LC * h + LC], held(nm) + ["nl%d" % t], ["c%s%d%d" % (nm, t, h)])
             ts(T["pk%d" % t][:, :], T.base[:, LC * t:LC * t + LC], cnt, A.add, ["base%d" % t, "cnt%d" % t], ["pk%d" % t], 1.0 / SPAN, A.mult)
             for nm in "cs":
-                pick(nm, ("s%%s%d" % n, 0, NB), (both[nm] + "%.0s", 0, 2 * NB), T["pk%d" % t][:, :], ["c%s%d0" % (nm, t), "c%s%d1" % (nm, t), "pk%d" % t], ["snd%s%d" % (nm, n)])
+                pick(nm, ("s%%s%d" % n, 0, NB), ("b%%s%d" % t, 0, 2 * NB), T["pk%d" % t][:, :], pairs(nm) + ["pk%d" % t], ["snd%s%d" % (nm, n)])
             send(n)
-        else:
-            sign()
-            for q in "va":
-                order(q, ["land%d" % t], [])
-        sel, tl = T["sel%d" % t][:, 0:1], T["tl%d" % t]
-        ts(sel, cnt, T.thrf[:, t:t + 1], A.is_ge, ["cnt%d" % t, "thrf", "two"], ["sel%d" % t], two, A.add)
-        cp(tl[:, :], T.both[:, 2 * TC * t:2 * TC * (t + 1)].indirect(sel), ["sel%d" % t, "botha", "bothb%d" % t], ["tl%d" % t])
-        if t < R - 1:
+            if t == 0:
+                ready(0)
+            sel = T["sel%d" % t][:, 0:1]
+            ts(sel, cnt, T.thrf[:, t:t + 1], A.is_ge, ["cnt%d" % t, "thrf", "two"], ["sel%d" % t], two, A.add)
+            cp(tl[:, :], T.both[:, 2 * TC * t:2 * TC * (t + 1)].indirect(sel), ["sel%d" % t, "botha", "bothb%d" % t], ["tl%d" % t])
             for nm in "cs":
                 pick(nm, ("l%%s%d" % n, 0, K), win, tl[:, :], held(nm) + ["tl%d" % t], ["tab%s%d" % (nm, n)])
-            pack(t)
-            ready(n)
-            if t == R - 2:
-                pack(n)
+            if n + 1 < R:
+                fetch(n + 1, ["tabc%d" % n])
             for o in range(O):
                 i = O * t + o
                 pb = 512 * (i % 4)
@@ -325,12 +320,29 @@ def rank_program(g, core, T, topo):
                     cp(T.ty[:, K * i:K * i + K], T.prod[:, pb:pb + K], ["prod%d" % (i % 4)], ["ty%d" % i])
             y = slice(O * K * t, O * K * (t + 1))
             dma("s", "yo%d" % t, T.y[:, y], T.ty[:, y], ["ty%d" % (O * t), "ty%d" % (O * t + 1)], ["out%d" % t])
-            if n + 1 < R:
-                fetch(n + 1, [])
+            if n < R - 1:
+                ready(n)
+            else:
+                for nm in "cs":
+                    pick(nm, ("b%%s%d" % n, 0, K), win, tl[:, :], held(nm) + ["tl%d" % t], ["old" + nm])
+            pack(n)
+            if t == 1:
+                v = T.bl[:, TC * (R - 1):TC * R]
+                l0, l1, l2, l3, l4 = (T.last[:, TC * i:TC * i + TC] for i in range(5))
+                ca, cb = (T.last[:, 5 * TC + i:5 * TC + i + 1] for i in range(2))
+                ts(ca, T.thrg[:, R - 1:R], -float(SPAN // 2 + 1), A.add, ["thrg"], ["ca"])
+                ts(cb, T.thrg[:, R - 1:R], -float(SPAN * K), A.add, ["thrg"], ["cb"])
+                ts(l0, v, float(K + B * r), A.is_ge, ["bl1"], ["l0"], float(B), A.mult)
+                ts(l1, v, float(SPAN), A.mult, ["bl1", "ca"], ["l1"], ca, A.add)
+                tt(l2, v, l0, A.add, ["bl1", "l0"], ["l2"])
+            if t == 2:
+                ts(l3, l2, float(2 * SPAN), A.mult, ["l2", "cb"], ["l3"], cb, A.add)
+                tt(l4, l1, l3, A.max, ["l1", "l3"], ["l4"])
         else:
+            ts(tl[:, :], l4, cnt, A.add, ["l4", "cnt%d" % t], ["tl%d" % t], 1.0 / SPAN, A.mult)
             for h in range(2):
                 for nm in "cs":
-                    pick(nm, ("l%%s%d" % n, H * h, H * h + H), win, tl[:, TC // 2 * h:TC // 2 * (h + 1)], held(nm) + ["tl%d" % t], ["tab%s%d%d" % (nm, n, h)])
+                    pick(nm, ("l%%s%d" % n, H * h, H * h + H), ("b%%s%d" % t, 0, K + 2 * NB), tl[:, TC // 2 * h:TC // 2 * (h + 1)], pairs(nm) + ["old" + nm, "tl%d" % t], ["tab%s%d%d" % (nm, n, h)])
                 for o in range(O):
                     i = O * t + o
                     pb = 512 * (2 * h + o)

@@ -4,13 +4,19 @@ from concourse.mybir import dt, AluOpType, ActivationFunctionType
 N, K, B, R, O = 8, 256, 12, 5, 2
 NB = N * B
 NEW = (N - 1) * B
-END = K + NEW
+PAD = 16 - B
+END = K + PAD + NEW
 LC = NB // 16
 TC = K // 16
-AL = R * LC
 WIN = K + 16
+HEAD = 32
+PAIRS = HEAD + 16 + 2 * NB
 SPAN = 512
 TINY = 1e-30
+TAIL = 96
+EARLY = 3
+FAR = True
+SPLIT = 4
 
 CODE, BYTE = "float8_e4m3fn_x4", "uint8"
 F32, I32, U16 = "float32", "int32", "uint16"
@@ -19,22 +25,24 @@ SCRATCH = {
     "ut": ("sbuf", [128, 512], "bfloat16"),
     "wt": ("sbuf", [128, 512 * R * O], "bfloat16"),
     "csl": ("sbuf", [128, LC], I32), "cdg": ("sbuf", [128, LC], I32), "csg": ("sbuf", [128, LC], I32),
-    "last": ("sbuf", [128, 5 * TC + 2], F32),
-    "cs0": ("sbuf", [128, LC], U16),
-    "thr1": ("sbuf", [1, 16], I32), "thri": ("sbuf", [128, 16], I32), "thrf": ("sbuf", [128, 16], F32),
-    "pp": ("sbuf", [128, 2], I32), "p16": ("sbuf", [128, 2], I32),
-    "colf": ("sbuf", [128, 8], F32),
-    "jc": ("sbuf", [128, R * TC], F32),
-    "ent": ("sbuf", [128, LC], F32),
-    "thrg": ("sbuf", [128, 16], F32), "base": ("sbuf", [128, R * LC], F32),
-    "pat": ("sbuf", [128, 32], F32), "turn": ("sbuf", [128, 32], U16),
+    "csu": ("sbuf", [128, 8], U16),
+    "last": ("sbuf", [128, TC], F32),
+    "thr1": ("sbuf", [1, 16], I32), "thri": ("sbuf", [128, 16], I32),
+    "thrf": ("sbuf", [128, 16], F32), "thrp": ("sbuf", [128, 16], F32),
+    "j0": ("sbuf", [128, 16], I32), "jt": ("sbuf", [128, 16], I32), "turn": ("sbuf", [128, 16], U16),
+    "colf": ("sbuf", [128, 12], F32),
+    "jc": ("sbuf", [128, (R - 1) * TC], F32),
+    "ent": ("sbuf", [128, N + 1], F32), "base": ("sbuf", [128, R * (N + 1)], F32),
     "cdo": ("sbuf", [128, LC], U16), "cso": ("sbuf", [128, LC], U16),
-    "vrow": ("sbuf", [128, NB], F32), "grow": ("sbuf", [128, 2 * NB + 32], F32),
-    "row": ("sbuf", [128, WIN], F32), "keys": ("sbuf", [128, K], F32),
-    "trow": ("sbuf", [128, K], F32), "srow": ("sbuf", [128, 256], U16),
-    "bl": ("sbuf", [128, R * TC], F32), "nl": ("sbuf", [128, 16 * R], U16),
-    "both": ("sbuf", [128, 2 * R * TC], F32),
+    "vrow": ("sbuf", [128, NB], F32), "vro2": ("sbuf", [128, NB], F32),
+    "gr": ("sbuf", [128, WIN + K], F32), "keys": ("sbuf", [128, WIN], F32),
+    "srow": ("sbuf", [128, K], U16), "trow": ("sbuf", [128, K], F32),
+    "nl": ("sbuf", [128, 16 * R], U16), "bl": ("sbuf", [128, TC * R], F32),
+    "both": ("sbuf", [128, 2 * (R - 1) * TC], F32),
     "zeros": ("sbuf", [128, 8], U16),
+    "bit": ("sbuf", [128, NEW], "bfloat16"),
+    "num": ("sbuf", [128, 4 * R], F32),
+    "dec": ("sbuf", [128, 4 * R], F32),
     "uc": ("sbuf", [128, 128], CODE), "us": ("sbuf", [128, 128], BYTE),
     "vc": ("sbuf", [128, 128], CODE), "vs": ("sbuf", [128, 128], BYTE),
     "wc": ("sbuf", [128, 128 * R * O], CODE), "ws": ("sbuf", [128, 128 * R * O], BYTE),
@@ -44,42 +52,43 @@ SCRATCH = {
     "prod": ("psum", [128, 2048], F32),
 }
 for _t in range(R + 1):
-    SCRATCH["lc%d" % _t] = ("sbuf", [128, END if _t < R else K], CODE)
-    SCRATCH["ls%d" % _t] = ("sbuf", [128, END if _t < R else K], BYTE)
+    for _n, _d in (("c", CODE), ("s", BYTE)):
+        SCRATCH["l%s%d" % (_n, _t)] = ("sbuf", [128, END if _t < R else K], _d)
+        if _t < R:
+            SCRATCH["s%s%d" % (_n, _t)] = ("sbuf", [128, 160], _d)
+            SCRATCH["b%s%d" % (_n, _t)] = ("sbuf", [128, PAIRS + (K if _t == R - 1 else 0)], _d)
+        if 0 < _t < R:
+            SCRATCH["p%s%d" % (_n, _t)] = ("sbuf", [128, 2 * B], _d)
 for _t in range(R):
-    SCRATCH["sc%d" % _t] = ("sbuf", [128, NB], CODE)
-    SCRATCH["ss%d" % _t] = ("sbuf", [128, NB], BYTE)
-    SCRATCH["bit%d" % _t] = ("sbuf", [128, NEW], "bfloat16")
-    SCRATCH["num%d" % _t] = ("sbuf", [128, 2], F32)
-    SCRATCH["sel%d" % _t] = ("sbuf", [128, 2], U16)
+    SCRATCH["pof%d" % _t] = ("sbuf", [128, 2], U16)
     SCRATCH["tl%d" % _t] = ("sbuf", [128, TC], U16)
-    SCRATCH["pk%d" % _t] = ("sbuf", [128, LC], U16)
-    SCRATCH["bc%d" % _t] = ("sbuf", [128, 2 * NB + (K if _t == R - 1 else 0)], CODE)
-    SCRATCH["bs%d" % _t] = ("sbuf", [128, 2 * NB + (K if _t == R - 1 else 0)], BYTE)
+    SCRATCH["pk%d" % _t] = ("sbuf", [128, N + 2], U16)
 
-SEMAPHORES = ["vq", "aq", "pq", "gq", "lx0", "lx1", "lcs", "lcd", "lu", "lt", "yp", "lb0", "lb1", "ln0", "ln1", "lcn"]
+SEMAPHORES = ["vq", "aq", "pq", "gq", "lx0", "lx1", "lcs", "lcd", "lu", "lt", "yp", "lcn", "lo", "left", "begun"]
 for _t in range(R):
-    SEMAPHORES += ["snt%d" % _t, "arr%d" % _t, "yo%d" % _t, "lw%d" % _t]
+    SEMAPHORES += [_n + str(_t) for _n in ("ln", "lb", "arr", "yo", "lw") + ("par", "dec") * min(_t, 1)]
 
 
-def deal(topo, cores, s):
+def roads(topo, cores, s):
     src = cores[s]
     here = topo.chip(src)
     way = lambda c: 2 if topo.mates(here, c) else 1 if topo.same_plane(here, c) else 0
     chips = sorted({topo.chip(c) for c in cores} - {here}, key=way)
-    on = lambda c: [d for d in range(len(cores)) if d != s and topo.chip(cores[d]) == c]
+    on = lambda c: sorted((d for d in range(len(cores)) if d != s and topo.chip(cores[d]) == c), key=lambda d: topo.die(cores[d]) == topo.die(src))
     bits = lambda es: sum(1 << e for e in es)
-    calls = []
-    for c in chips:
-        ds = on(c)
-        eng = topo.engines(src, cores[ds[0]])
-        for h, nm in enumerate("cs"):
-            m = {d: bits(eng[i::len(ds)]) for i, d in enumerate(ds)}
-            if c == chips[-1]:
-                for d in on(here):
-                    m[d] = bits([e for e in topo.engines(src, cores[d]) if e not in eng][2 * h::4])
-            calls.append((nm, m))
-    return calls
+    (near,), (partner, second) = on(here), on(chips[0 if FAR else -1])
+    out = topo.engines(src, cores[partner])
+    share = lambda ds: {d: bits(out[i::len(ds)]) for i, d in enumerate(ds)}
+    first = [share(on(c)) for c in chips]
+    later = [share([d for d in on(c) if d != partner]) for c in chips]
+    first[1][near] = later[1][near] = bits([e for e in topo.engines(src, cores[near]) if e not in out])
+    return {"first": first, "later": later, "partner": partner, "out": bits(out)}
+
+
+def landing(road, d, s, t):
+    turn = [(road[d]["partner"] + i) % N for i in range(N)]
+    turn.remove(d)
+    return K + (PAD if t else 0) + B * turn.index(s)
 
 
 def rank_program(g, core, T, topo):
@@ -87,8 +96,10 @@ def rank_program(g, core, T, topo):
     if r is None:
         return
     cores = list(T.cores)
+    road = [roads(topo, cores, s) for s in range(N)]
     A, F = AluOpType, ActivationFunctionType
-    plans = [deal(topo, cores, s) for s in range(N)]
+    me = road[r]
+    mate = me["partner"]
     ones = lambda m: bin(m).count("1")
 
     total, W, RD = {}, {}, {}
@@ -102,7 +113,7 @@ def rank_program(g, core, T, topo):
             n = total[sem] if n is None else n
             if qs[q]["seen"].get(sem, 0) < n:
                 need[sem] = max(need.get(sem, 0), n)
-        for sem in sorted(need, key=lambda s: (s.startswith("arr"), s)):
+        for sem in sorted(need, key=lambda s: (s[:3] in ("arr", "par", "dec"), s)):
             qs[q]["eng"].wait_ge(T.sem[sem], need[sem])
             qs[q]["seen"][sem] = need[sem]
 
@@ -145,86 +156,100 @@ def rank_program(g, core, T, topo):
         else:
             do("v", lambda e: e.tensor_scalar(out, in0, s1, s2, op0, op1), rd, wr)
 
-    def tt(out, in0, in1, op, rd, wr):
-        do("v", lambda e: e.tensor_tensor(out, in0, in1, op), rd, wr)
-
     def cp(out, in_, rd, wr):
         do("v", lambda e: e.tensor_copy(out, in_), rd, wr)
 
+    def act(out, in_, rd, wr, func=F.Copy, **kw):
+        do("a", lambda e: e.activation(out, in_, func, **kw), rd, wr)
+
     for t in range(R):
-        total["arr%d" % t] = sum(ones(m.get(r, 0)) for plan in plans for _nm, m in plan)
+        total["arr%d" % t] = 2 * sum(ones(m[r]) for o in road for m in o["later" if t else "first"] if r in m)
         W["land%d" % t] = [("arr%d" % t, None)]
+        if t:
+            total["par%d" % t], total["dec%d" % t] = 2 * ones(road[mate]["out"]), ones(road[mate]["out"])
+            W["pair%d" % t], W["dec%d" % t] = [("par%d" % t, None)], [("dec%d" % t, None)]
 
     h = 2 * K
     dma("s", "lx0", T.xt[:, 0:h], T.x[:, 0:h], [], ["x0"])
     for i in range(8):
         dma("a" if i < 5 else "s", "lcs", T.csl[16 * i:16 * i + 16, :], T.cs[:, 0:LC], [], ["cs"])
-    dma("a", "lt", T.thr1[0:1, :], T.thr[:, :], [], ["thr1"])
     dma("s", "lx1", T.xt[:, h:2 * h], T.x[:, h:2 * h], [], ["x1"])
     for i in range(8):
         t = min(i, R - 1)
-        dma("sa"[i % 2], "lcd", T.cdg[16 * i:16 * i + 16, :], T.cd[:, LC * t:LC * t + LC], [], ["cd"])
+        dma("as"[i % 2], "lcd", T.cdg[16 * i:16 * i + 16, :], T.cd[:, LC * t:LC * t + LC], [], ["cd"])
     for i in range(8):
         src = T.cs[:, LC * (i + 1):LC * (i + 2)] if i < R - 1 else T.cd[:, LC * (R - 1):LC * R]
-        dma("sa"[i % 2], "lcn", T.csg[16 * i:16 * i + 16, :], src, [], ["csg"])
+        dma("as"[i % 2], "lcn", T.csg[16 * i:16 * i + 16, :], src, [], ["csg"])
+    dma("a", "lt", T.thr1[0:1, :], T.thr[:, :], [], ["thr1"])
     dma("s", "lu", T.ut[:, 0:8], T.u[:, 0:8], [], ["u"])
 
     fl = {"allow_small_or_imprecise_dtypes": True}
-    do("g", lambda e: e.iota(T.pp[:, 0:1], [[0, 1]], 0, 1), [], ["pp"])
-    do("g", lambda e: e.iota(T.jc[:, :], [[0, R], [16, TC]], 0, 0, **fl), [], ["jc"])
-    do("g", lambda e: e.iota(T.pat[:, 0:16], [[1, 8], [NB, 2]], 0, 0, **fl), [], ["pata"])
-    do("g", lambda e: e.iota(T.pat[:, 16:32], [[1, 16]], 0, 0, **fl), [], ["patb"])
-    do("g", lambda e: e.iota(T.row[:, :], [[1, WIN]], 0, 0, **fl), [], ["row"])
-    do("g", lambda e: e.iota(T.vrow[:, 0:B * (r + 1)], [[1, B * (r + 1)]], K, 0, **fl), [], ["vrowa"])
-    W["vrowb"] = []
-    if r < N - 1:
-        do("g", lambda e: e.iota(T.vrow[:, B * (r + 1):NB], [[1, NB - B * (r + 1)]], K + B * r, 0, **fl), [], ["vrowb"])
-    do("v", lambda e: e.memset(T.zeros[:, :], 0), [], ["zeros"])
+    row = T.gr[:, 0:WIN]
+    lead = 16 * (2 * B * mate // 16 % 2)
+    mine = (lead + 2 * B * mate) // 16
+    do("g", lambda e: e.iota(T.j0[:, :], [[1, 16]], 0, 16), [], ["j0"])
+    do("g", lambda e: e.iota(T.keys[:, 0:WIN // 2], [[1, WIN // 2]], 0, 0, **fl), [], ["keya"])
+    runs = []
+    for s in range(N):
+        at = None if s == r else landing(road, r, s, 0) - B * s
+        if runs and at in (None, runs[-1][2]):
+            runs[-1][1] = s + 1
+        elif runs and runs[-1][2] is None:
+            runs[-1][1:] = [s + 1, at]
+        else:
+            runs.append([s, s + 1, at])
+    for a, b, at in runs:
+        do("g", lambda e: e.iota(T.vrow[:, B * a:B * b], [[1, B * (b - a)]], at + B * a, 0, **fl), [], ["vrow%d" % a])
     do("v", lambda e: e.memset(T.ut[:, 8:512], 0.0), [], ["u0"])
-    do("v", lambda e: e.memset(T.grow[:, 2 * NB:], 0.0), [], ["growc"])
-    pi = T.p16[:, 0:1]
-    ts(pi, T.pp[:, 0:1], 15, A.bitwise_and, ["pp"], ["p16"])
-    p16, two, p8x, p16x, cap = (T.colf[:, i:i + 1] for i in range(5))
-    cp(p16, pi, ["p16"], ["p16f"])
-    ts(two, pi, 2.0, A.mult, ["p16"], ["two"])
-    ts(p8x, pi, 8.0, A.mult, ["p16"], ["p8x"])
-    ts(p16x, pi, 16.0, A.mult, ["p16"], ["p16x"])
-    ts(cap, pi, float(K), A.add, ["p16"], ["cap"])
+    do("v", lambda e: e.memset(T.gr[:, WIN + lead + 2 * NB:], 0.0), [], ["rest"])
+    W["lead"] = []
+    if lead:
+        do("v", lambda e: e.memset(T.gr[:, WIN:WIN + lead], 0.0), [], ["lead"])
+    p16, back, p16x, cap, late, pm, pq = (T.colf[:, i:i + 1] for i in range(7))
+    ts(T.jt[:, :], T.j0[:, :], K - 1, A.bitwise_and, ["j0"], ["jt"])
+    ts(late, T.j0[:, 0:1], float(K), A.is_ge, ["j0"], ["late"], float(PAD), A.mult)
+    q16 = T.jt[:, 0:1]
+    cp(T.turn[:, :], T.jt[:, :], ["jt"], ["turn"])
+    ts(cap, q16, 1.0 / 16, A.mult, ["jt"], ["cap"], float(K), A.add)
     own = {}
     for c in range(LC):
         lo, hi = max(B * r - 16 * c, 0), min(B * r + B - 16 * c, 16)
         if lo < hi:
-            own[c] = T.colf[:, 6 + len(own):7 + len(own)]
-            ts(own[c], pi, 0.5 - (lo or hi), A.add, ["p16"], ["own%d" % c], 4.0 * K * (1 if lo else -1), A.mult)
-    ts(T.turn[:, 0:16], T.pat[:, 0:16], p8x, A.add, ["pata", "p8x"], ["turna"])
-    ts(T.turn[:, 16:32], T.pat[:, 16:32], p16x, A.add, ["patb", "p16x"], ["turnb"])
-    ts(T.both[:, 0:2 * R * TC:2], T.jc[:, :], p16, A.add, ["jc", "p16f"], ["botha"])
-    ts(T.ent[:, :], T.jc[:, 0:LC], p16, A.add, ["jc", "p16f"], ["ent"], float(2 * SPAN), A.mult)
-    do("a", lambda e: e.activation(T.keys[:, :], T.row[:, 0:K], F.Copy), ["row"], ["keys"])
+            own[c] = T.colf[:, 8 + len(own):9 + len(own)]
+            ts(own[c], q16, 8.0 - 16 * (lo or hi), A.add, ["jt"], ["own%d" % c], K / 4.0 * (1 if lo else -1), A.mult)
+    act(T.keys[:, WIN // 2:], T.keys[:, 0:WIN // 2], ["keya"], ["keys"], F.Identity, bias=float(WIN // 2))
+    act(T.vro2[TAIL:, :], T.keys[TAIL:, 0:NB], ["keya"], ["vro3"], F.Identity, bias=K + HEAD + lead + (SPAN // 2 + 1) / SPAN, scale=2.0)
+    act(row, T.keys[:, :], ["keya", "keys"], ["row"])
+    act(T.vro2[0:TAIL, :], T.vrow[0:TAIL, :], ["late"] + ["vrow%d" % a for a, _b, _c in runs], ["vro2"], F.Identity, bias=T.colf[0:TAIL, 4:5])
 
     def pick(nm, out, win, off, rd, wr):
         o, w = T[out[0] % nm][:, out[1]:out[2]], T[win[0] % nm][:, win[1]:win[2]]
         if nm == "c":
             do("v", lambda e: e.tensor_copy(o.bitcast(dt.uint32), w.bitcast(dt.uint32).indirect(off)), rd, wr)
         else:
-            do("a", lambda e: e.activation(o, w.indirect(off), F.Copy), rd, wr)
+            act(o, w.indirect(off), rd, wr)
 
-    def send(t):
-        for nm, m in plans[r]:
-            order("g", ["snd%s%d" % (nm, t)], [])
-            moves = []
-            for d in sorted(m):
-                rid, pid, _ring = topo.addr(cores[d])
-                a = K + B * (r - (r > d))
-                src = T["s%s%d" % (nm, t)][:, B * d:B * d + B]
-                dst = T["l%s%d" % (nm, t)][:, a:a + B]
-                if nm == "c":
-                    src, dst = src.bitcast(dt.uint8), dst.bitcast(dt.uint8)
-                moves.append(RemoteDMATransfer(dst_ids=[DstId(rid=rid, pnc=pid)], dma_engine_mask=m[d], remote_sem=T.sem["arr%d" % t], src=src, dst=dst))
-            sem = "snt%d" % t
-            g.remote_dma_fused(moves, local_sem=T.sem[sem])
-            total[sem] = total.get(sem, 0) + sum(ones(m[d]) for d in m)
-        W["sent%d" % t] = [(sem, None)]
+    def write(d, mask, sem, src, dst):
+        rid, pid, _ring = topo.addr(cores[d])
+        return RemoteDMATransfer(dst_ids=[DstId(rid=rid, pnc=pid)], dma_engine_mask=mask, remote_sem=T.sem[sem], src=src, dst=dst), ones(mask)
+
+    def cols(nm, name, a, n):
+        v = T[name % nm][:, a:a + n]
+        return v.bitcast(dt.uint8) if nm == "c" else v
+
+    def call(moves, sem, rd):
+        order("g", rd, [])
+        g.remote_dma_fused([m for m, _n in moves], local_sem=T.sem[sem])
+        total[sem] = total.get(sem, 0) + sum(n for _m, n in moves)
+
+    def send(t, where):
+        for m in me["later" if t else "first"]:
+            for nm in "cs":
+                moves = [write(d, m[d], "arr%d" % t, cols(nm, "s%%s%d" % t, where[d][0], B), cols(nm, "l%%s%d" % t, landing(road, d, r, t), B)) for d in m]
+                call(moves, "begun" if t == 0 and m is me["first"][0] else "left", ["snd%s%d%d" % (nm, t, where[d][1]) for d in m])
+        W["begun"] = [("begun", None)]
+
+    held = lambda x, t: ["tab%s%d" % (x, t), "land%d" % t] + ["got%s%d" % (x, t)] * min(t, 1)
 
     def fetch(t, rd):
         a, b = 512 * O * t, 512 * O * (t + 1)
@@ -234,17 +259,45 @@ def rank_program(g, core, T, topo):
         a, b = 128 * O * t, 128 * O * (t + 1)
         do("v", lambda e: e.quantize_mx(T.wc[:, a:b], T.ws[:, a:b], T.wt[:, 4 * a:4 * b]), ["w%d" % t], ["wq%d" % t])
 
-    fetch(0, [])
-    fetch(1, [])
-    do("g", lambda e: e.partition_broadcast(T.thri[:, :], T.thr1[0:1, :], 128), ["thr1"], ["thri"])
+    def unload(t):
+        for o in range(O):
+            i = O * t + o
+            pb = 512 * (i % 4)
+            (act if o else cp)(T.ty[:, K * i:K * i + K], T.prod[:, pb:pb + K], ["prod%d" % (i % 4)], ["ty%d" % i])
+
+    def store(t, rd):
+        y = slice(O * K * t, O * K * (t + 1))
+        dma("s", "yo%d" % t, T.y[:, y], T.ty[:, y], ["ty%d" % (O * t), "ty%d" % (O * t + 1)] + rd, ["out%d" % t])
+
+    def lists(t, rd):
+        p = 16 * t if t < R - 1 else TAIL
+        dma("s", "ln%d" % t, T.nl[:, 16 * t:16 * t + 16], T.srow[16 * t:16 * t + 8, :], ["srow"] + rd, ["nl%d" % t])
+        dma("s", "lb%d" % t, T.bl[:, 16 * t:16 * t + 16], T.trow[p:p + 8, :], ["trow"], ["bl%d" % t])
+
+    def ready(t):
+        bl = T.bl[:, TC * t:TC * t + TC]
+        if t < R - 1:
+            act(T.both[:, 2 * TC * t + 1:2 * TC * (t + 1):2], bl, ["bl%d" % t, "botha"], ["bothb%d" % t])
+        else:
+            act(T.last[:, :], bl, ["bl%d" % t, "back"], ["last"], F.Identity, bias=back, scale=float(SPAN))
+
+    for t in range(EARLY):
+        fetch(t, [])
+    far = sorted(me["first"][0])
+    a, b = B * far[0] // 16, (B * far[-1] + B + 15) // 16
     H = K // 2
     for i in range(2):
         do("v", lambda e: e.quantize_mx(T.xc[:, H * i:H * i + H], T.xs[:, H * i:H * i + H], T.xt[:, 4 * H * i:4 * H * (i + 1)]), ["x%d" % i], ["xq%d" % i])
         if i == 0:
-            cp(T.cs0[:, :], T.csl[:, 0:LC], ["cs"], ["cs0"])
-    for nm in "cs":
-        pick(nm, ("s%s0", 0, NB), ("x%s", 0, K), T.cs0[:, :], ["xq0", "xq1", "cs0"], ["snd%s0" % nm])
-    send(0)
+            cp(T.csu[:, 0:LC], T.csl[:, :], ["cs"], ["csu0"])
+            if a % 2:
+                cp(T.csu[:, LC:LC + b - a], T.csl[:, a:b], ["cs"], ["csu1"])
+    where = {d: (32 + B * d, 1) for d in range(N)}
+    where.update({d: (B * d - 16 * a, 0) for d in far})
+    for i, (to, off, rd) in enumerate(((0, T.csu[:, LC:LC + b - a] if a % 2 else T.csu[:, a:b], "csu%d" % (a % 2)), (32, T.csu[:, 0:LC], "csu0"))):
+        for nm in "cs":
+            pick(nm, ("s%s0", to, to + (NB if i else 16 * (b - a))), ("x%s", 0, K), off, ["xq0", "xq1", rd], ["snd%s0%d" % (nm, i)])
+    send(0, where)
 
     here = []
     for c in range(LC):
@@ -256,93 +309,106 @@ def rank_program(g, core, T, topo):
             cp(T.cdo[:, a:b], T.cdg[:, a:b], ["cd"], ["cdo%d" % a])
             here.append("cdo%d" % a)
     cp(T.cso[:, :], T.csg[:, :], ["csg"], ["cso"])
+    cp(row.indirect(T.cdo[:, :]), T.vro2[:, :], here + ["vro2", "vro3"], ["row"])
+    a = WIN + lead
+    act(T.gr[:, a:a + 2 * NB:2], T.keys[:, :].indirect(T.cso[:, :]), ["keys", "cso"], ["grow"])
+    cp(T.gr[:, a + 1:a + 2 * NB:2], row.indirect(T.cso[:, :]), ["cso", "row"], ["grow"])
+    act(T.trow[:, :], row.indirect(T.turn[:, :]), ["row", "turn"], ["trow"])
+    cp(T.srow[:, :], T.gr[:, WIN:].indirect(T.turn[:, :]), ["grow", "lead", "rest", "turn"], ["srow"])
+    lists(0, [])
+    lists(1, ["begun"])
+    fetch(EARLY, ["begun"])
+    SEL, PC = N, N + 1
+    do("g", lambda e: e.iota(T.ent[:, 0:N], [[2 * SPAN * B, N]], SPAN * (HEAD + lead), 0, **fl), [], ["enta"])
+    do("g", lambda e: e.iota(T.jc[:, :], [[0, R - 1], [16, TC]], 0, 0, **fl), [], ["jc"])
+    do("g", lambda e: e.partition_broadcast(T.thri[:, :], T.thr1[0:1, :], 128), ["thr1", "jc"], ["thri"])
+    do("v", lambda e: e.memset(T.zeros[:, :], 0), [], ["zeros"])
+    cp(p16x, q16, ["jt"], ["p16x"])
     do("v", lambda e: e.quantize_mx(T.uc[:, :], T.us[:, :], T.ut[:, :]), ["u", "u0"], ["uq"])
-    cp(T.row[:, :].indirect(T.cdo[:, :]), T.vrow[:, :], here + ["vrowa", "vrowb"], ["row"])
-    do("a", lambda e: e.activation(T.grow[:, 0:NB], T.keys[:, :].indirect(T.cso[:, 0:LC]), F.Copy), ["keys", "cso"], ["growa"])
-    pick("c", ("v%s", 0, 128), ("u%s", 0, 128), T.zeros[:, :], ["uq", "zeros"], ["vc"])
-    cp(T.grow[:, NB:2 * NB], T.row[:, :].indirect(T.cso[:, 0:LC]), ["cso", "row"], ["growb"])
-    do("a", lambda e: e.activation(T.trow[:, :], T.row[:, :].indirect(T.turn[:, 16:32]), F.Copy), ["row", "turnb"], ["trow"])
-    pick("s", ("v%s", 0, 128), ("u%s", 0, 128), T.zeros[:, :], ["uq", "zeros"], ["vs"])
+    ts(pm, q16, 16.0 * (B - 1), A.min, ["jt"], ["pm"], SPAN / 8.0, A.mult)
+    for nm in "cs":
+        pick(nm, ("v%s", 0, 128), ("u%s", 0, 128), T.zeros[:, :], ["uq", "zeros"], ["v" + nm])
     do("v", lambda e: e.quantize_mx(T.lc0[:, 0:K], T.ls0[:, 0:K], T.xt[:, :]), ["x0", "x1"], ["tabc0", "tabs0"])
-    cp(T.srow[:, :], T.grow[:, :].indirect(T.turn[:, 0:16]), ["growa", "growb", "growc", "turna"], ["srow"])
-    for t in range(R):
-        n = min(t, 1)
-        if True:
-            dma("s", "ln%d" % n, T.nl[:, 16 * t:16 * t + 16], T.srow[16 * t:16 * t + 8, :], ["srow"] + ["sent0"] * n, ["nl%d" % n])
-        dma("s", "lb%d" % n, T.bl[:, TC * t:TC * t + TC], T.trow[16 * t:16 * t + 8, :], ["trow"], ["bl%d" % n])
-    ts(T.thrg[:, :], T.thri[:, :], -2.0, A.mult, ["thri"], ["thrg"], float(NEW + SPAN // 2 + 1), A.add)
     ts(T.thrf[:, :], T.thri[:, :], 2.0, A.mult, ["thri"], ["thrf"], float(-NEW), A.add)
+    ts(T.thrp[:, :], T.thri[:, :], -2.0, A.mult, ["thri", "pm"], ["thrp"], pm, A.add)
+    half = float(NEW + SPAN // 2 + 1)
+    act(T.ent[:, SEL:PC], p16x, ["p16x"], ["entb"], F.Relu, bias=-2.0 * SPAN * (B - 1), scale=SPAN / 8.0)
+    act(p16, p16x, ["p16x"], ["p16f"], scale=1.0 / 16)
+    act(pq, p16x, ["p16x"], ["pq"], F.Relu, bias=-2.0 * PAD, scale=1.0 / 8)
+    act(T.ent[:, :], T.ent[:, :], ["enta", "entb"], ["ent"], F.Identity, bias=half)
+    act(T.both[:, 0:2 * (R - 1) * TC:2], T.jc[:, :], ["jc", "p16f"], ["botha"], F.Identity, bias=p16)
+    act(back, T.thrf[:, R - 1:R], ["thrf"], ["back"], scale=-1.0)
     for t in range(R - 1):
-        ts(T.base[:, LC * t:LC * t + LC], T.ent[:, :], T.thrg[:, t:t + 1], A.add, ["ent", "thrg"], ["base%d" % t])
+        act(T.base[:, PC * t:PC * t + PC], T.ent[:, :], ["thrp", "ent"], ["base%d" % t], F.Identity, bias=T.thrp[:, t:t + 1])
     pack(0)
-
-    def ready(t):
-        cp(T.both[:, 2 * TC * t + 1:2 * TC * (t + 1):2], T.bl[:, TC * t:TC * t + TC], ["bl%d" % min(t, 1)], ["bothb%d" % t])
+    pack(1)
+    slot, picks = {}, []
+    for ms in (me["later"][:1], me["later"][1:]):
+        ds = [d for m in ms for d in m if d not in slot]
+        a, b, to = min(ds) // 2 * 2, max(ds) + 1, 32 * len(picks)
+        slot.update({d: (to + 16 * (d - a), len(picks)) for d in range(a, b) if d not in slot})
+        picks.append((a, b, to))
 
     for t in range(R):
         n = t + 1
-        held = lambda x: ["tab%s%d" % (x, t), "land%d" % t]
+        end = END if t else END - PAD
         win = ("l%%s%d" % t, 0, END)
         sb = 512 * (t % 2)
-        cnt = T["num%d" % t][:, 0:1]
-        do("p", lambda e: e.matmul_mx(T.acc[:, sb:sb + 128], T.vc[:, :], T.vs[:, :], T["lc%d" % t][:, END - 128:END], T["ls%d" % t][:, END - 128:END], True, True), ["vc", "vs"] + held("c") + held("s"), ["acc%d" % (t % 2)])
-        sign = lambda: do("a", lambda e: e.activation(T["bit%d" % t][:, :], T.acc[:, sb + 128 - NEW:sb + 128], F.Sign, bias=TINY, accum_out=cnt), ["acc%d" % (t % 2)], ["cnt%d" % t])
-        first, tl = (0 if t < R - 1 else K), T["tl%d" % t]
+        cnt = T.num[:, 4 * t:4 * t + 1]
+        do("p", lambda e: e.matmul_mx(T.acc[:, sb:sb + 128], T.vc[:, :], T.vs[:, :], T["lc%d" % t][:, end - 128:end], T["ls%d" % t][:, end - 128:end], True, True), ["vc", "vs"] + held("c", t) + held("s", t), ["acc%d" % (t % 2)])
+        first, tl = (0 if n < R else K), T["tl%d" % t]
+        whole = 2 * LC + lead // 16
+        cuts = ((mine, mine + 2, 0), (0, whole, HEAD)) if n < R else ((0, SPLIT, HEAD), (SPLIT, whole, HEAD + 16 * SPLIT))
         for h, nm in ((0, "c"), (0, "s"), (1, "c"), (1, "s")):
             if (h, nm) == (1, "s"):
-                sign()
-            pick(nm, ("b%%s%d" % t, first + NB * h, first + NB * h + NB), win, T.nl[:, 16 * t + LC * h:16 * t + LC * h + LC], held(nm) + ["nl%d" % min(t, 1)], ["c%s%d%d" % (nm, t, h)])
+                act(T.bit[:, :], T.acc[:, sb + 128 - NEW:sb + 128], ["acc%d" % (t % 2)], ["cnt%d" % t, "bit"], F.Sign, bias=TINY, accum_out=cnt)
+            a, b, to = cuts[h]
+            pick(nm, ("b%%s%d" % t, first + to, first + to + 16 * (b - a)), win, T.nl[:, 16 * t + a:16 * t + b], held(nm, t) + ["nl%d" % t], ["c%s%d%d" % (nm, t, h)])
         pairs = lambda x: ["c%s%d0" % (x, t), "c%s%d1" % (x, t)]
-        if t < R - 1:
-            ts(T["pk%d" % t][:, :], T.base[:, LC * t:LC * t + LC], cnt, A.add, ["base%d" % t, "cnt%d" % t], ["pk%d" % t], 1.0 / SPAN, A.mult)
+        if n < R:
             for nm in "cs":
-                pick(nm, ("s%%s%d" % n, 0, NB), ("b%%s%d" % t, 0, 2 * NB), T["pk%d" % t][:, :], pairs(nm) + ["pk%d" % t], ["snd%s%d" % (nm, n)])
-            send(n)
+                call([write(mate, me["out"], "par%d" % n, cols(nm, "b%%s%d" % t, 2 * B * mate % 16, 2 * B), cols(nm, "p%%s%d" % n, 0, 2 * B))], "left", ["c%s%d0" % (nm, t)])
+            call([write(mate, me["out"], "dec%d" % n, cnt, T.dec[:, 4 * n:4 * n + 1])], "left", ["cnt%d" % t])
+            pk = T["pk%d" % t]
+            ts(pk[:, 0:PC], T.base[:, PC * t:PC * t + PC], cnt, A.add, ["base%d" % t, "cnt%d" % t], ["pk%d" % t], 1.0 / SPAN, A.mult)
+            for i, (a, b, to) in enumerate(picks):
+                for nm in "cs":
+                    pick(nm, ("s%%s%d" % n, to, to + 16 * (b - a)), ("b%%s%d" % t, 0, PAIRS), pk[:, a:b], pairs(nm) + ["pk%d" % t], ["snd%s%d%d" % (nm, n, i)])
+            send(n, slot)
             if t == 0:
                 ready(0)
-            sel = T["sel%d" % t][:, 0:1]
-            ts(sel, cnt, T.thrf[:, t:t + 1], A.is_ge, ["cnt%d" % t, "thrf", "two"], ["sel%d" % t], two, A.add)
-            cp(tl[:, :], T.both[:, 2 * TC * t:2 * TC * (t + 1)].indirect(sel), ["sel%d" % t, "botha", "bothb%d" % t], ["tl%d" % t])
+            pof = T["pof%d" % t][:, 0:1]
+            cp(tl[:, :], T.both[:, 2 * TC * t:2 * TC * (t + 1)].indirect(pk[:, SEL:SEL + 1]), ["pk%d" % t, "botha", "bothb%d" % t], ["tl%d" % t])
             for nm in "cs":
-                pick(nm, ("l%%s%d" % n, 0, K), win, tl[:, :], held(nm) + ["tl%d" % t], ["tab%s%d" % (nm, n)])
+                pick(nm, ("l%%s%d" % n, 0, K), win, tl[:, :], held(nm, t) + ["tl%d" % t], ["tab%s%d" % (nm, n)])
+            ts(pof, T.dec[:, 4 * n:4 * n + 1], T.thrf[:, t:t + 1], A.is_ge, ["dec%d" % n, "thrf", "pq"], ["pof%d" % t], pq, A.add)
+            for nm in "cs":
+                pick(nm, ("l%%s%d" % n, K, K + 16), ("p%%s%d" % n, 0, 2 * B), pof, ["pair%d" % n, "pof%d" % t], ["got%s%d" % (nm, n)])
+            under = ["pof%d" % t]
             if n + 1 < R:
-                fetch(n + 1, ["tabc%d" % n])
+                lists(n + 1, under)
+            if n + EARLY < R:
+                fetch(n + EARLY, under)
+            if n + 1 == R:
+                for nm in "cs":
+                    dma("s", "lo", cols(nm, "b%%s%d" % n, 0, K), cols(nm, "l%%s%d" % n, 0, K), ["tab%s%d" % (nm, n)] + under, ["kept"])
+            if t:
+                store(t - 1, under)
             for o in range(O):
                 i = O * t + o
                 pb = 512 * (i % 4)
                 do("p", lambda e: e.matmul_mx(T.prod[:, pb:pb + K], T.wc[:, 128 * i:128 * i + 128], T.ws[:, 128 * i:128 * i + 128], T["lc%d" % n][:, 0:K], T["ls%d" % n][:, 0:K], True, True), ["wq%d" % t, "tabc%d" % n, "tabs%d" % n], ["prod%d" % (i % 4)])
-            for o in range(O):
-                i = O * t + o
-                pb = 512 * (i % 4)
-                if o:
-                    do("a", lambda e: e.activation(T.ty[:, K * i:K * i + K], T.prod[:, pb:pb + K], F.Copy), ["prod%d" % (i % 4)], ["ty%d" % i])
-                else:
-                    cp(T.ty[:, K * i:K * i + K], T.prod[:, pb:pb + K], ["prod%d" % (i % 4)], ["ty%d" % i])
-            y = slice(O * K * t, O * K * (t + 1))
-            dma("s", "yo%d" % t, T.y[:, y], T.ty[:, y], ["ty%d" % (O * t), "ty%d" % (O * t + 1)], ["out%d" % t])
-            if n < R - 1:
-                ready(n)
-            else:
-                for nm in "cs":
-                    pick(nm, ("b%%s%d" % n, 0, K), win, tl[:, :], held(nm) + ["tl%d" % t], ["old" + nm])
-            pack(n)
-            if t == 1:
-                v = T.bl[:, TC * (R - 1):TC * R]
-                l0, l1, l2, l3, l4 = (T.last[:, TC * i:TC * i + TC] for i in range(5))
-                ca, cb = (T.last[:, 5 * TC + i:5 * TC + i + 1] for i in range(2))
-                ts(ca, T.thrg[:, R - 1:R], -float(SPAN // 2 + 1), A.add, ["thrg"], ["ca"])
-                ts(cb, T.thrg[:, R - 1:R], -float(SPAN * K), A.add, ["thrg"], ["cb"])
-                ts(l0, v, float(K + B * r), A.is_ge, ["bl1"], ["l0"], float(B), A.mult)
-                ts(l1, v, float(SPAN), A.mult, ["bl1", "ca"], ["l1"], ca, A.add)
-                tt(l2, v, l0, A.add, ["bl1", "l0"], ["l2"])
-            if t == 2:
-                ts(l3, l2, float(2 * SPAN), A.mult, ["l2", "cb"], ["l3"], cb, A.add)
-                tt(l4, l1, l3, A.max, ["l1", "l3"], ["l4"])
+            ready(n)
+            if n + 1 < R:
+                pack(n + 1)
+            unload(t)
+            if n + 1 == R:
+                store(t, [])
         else:
-            ts(tl[:, :], l4, cnt, A.add, ["l4", "cnt%d" % t], ["tl%d" % t], 1.0 / SPAN, A.mult)
+            ts(tl[:, :], T.last[:, :], cnt, A.add, ["last", "cnt%d" % t], ["tl%d" % t], 1.0 / SPAN, A.mult)
             for h in range(2):
                 for nm in "cs":
-                    pick(nm, ("l%%s%d" % n, H * h, H * h + H), ("b%%s%d" % t, 0, K + 2 * NB), tl[:, TC // 2 * h:TC // 2 * (h + 1)], pairs(nm) + ["old" + nm, "tl%d" % t], ["tab%s%d%d" % (nm, n, h)])
+                    pick(nm, ("l%%s%d" % n, H * h, H * h + H), ("b%%s%d" % t, 0, K + PAIRS), tl[:, TC // 2 * h:TC // 2 * (h + 1)], pairs(nm) + ["kept", "tl%d" % t], ["tab%s%d%d" % (nm, n, h)])
                 for o in range(O):
                     i = O * t + o
                     pb = 512 * (2 * h + o)
@@ -351,11 +417,11 @@ def rank_program(g, core, T, topo):
                 for o in range(O):
                     a, pb = K * (O * t + o) + H * h, 512 * (2 * h + o)
                     y = slice(a, a + H)
-                    if o:
-                        do("a", lambda e: e.activation(T.ty[:, y], T.prod[:, pb:pb + H], F.Copy), ["prod%d" % (2 * h + o)], ["tyz%d%d" % (h, o)])
-                    else:
-                        cp(T.ty[:, y], T.prod[:, pb:pb + H], ["prod%d" % (2 * h + o)], ["tyz%d%d" % (h, o)])
+                    (act if o else cp)(T.ty[:, y], T.prod[:, pb:pb + H], ["prod%d" % (2 * h + o)], ["tyz%d%d" % (h, o)])
                     q, sem = ("a", "yp") if o and h else ("s", "yo%d" % t)
                     dma(q, sem, T.y[:, y], T.ty[:, y], ["tyz%d%d" % (h, o)], ["outz%d%d" % (h, o)])
 
-    hold("g", [(sem, None) for sem in sorted(total)])
+    last = {"yp": "a", "yo%d" % (R - 1): "s", "aq": "a", "vq": "v", "pq": "p"}
+    for sem in sorted(total, key=lambda s: s == "yp"):
+        if all(q["seen"].get(sem, 0) < total[sem] for q in qs.values()):
+            hold(last.get(sem, "g"), [(sem, None)])

from concourse.bass import DstId, RemoteDMATransfer
from concourse.mybir import dt, AluOpType, ActivationFunctionType

N, K, B, R, O = 8, 256, 12, 5, 2
NB = N * B
NEW = (N - 1) * B
PAD = 16 - B
END = K + PAD + NEW
LC = NB // 16
TC = K // 16
WIN = K + 16
HEAD = 32
PAIRS = HEAD + 16 + 2 * NB
SPAN = 512
TINY = 1e-30
TAIL = 96
EARLY = 3
FAR = True
SPLIT = 4

CODE, BYTE = "float8_e4m3fn_x4", "uint8"
F32, I32, U16 = "float32", "int32", "uint16"
SCRATCH = {
    "xt": ("sbuf", [128, 4 * K], "bfloat16"),
    "ut": ("sbuf", [128, 512], "bfloat16"),
    "wt": ("sbuf", [128, 512 * R * O], "bfloat16"),
    "csl": ("sbuf", [128, LC], I32), "cdg": ("sbuf", [128, LC], I32), "csg": ("sbuf", [128, LC], I32),
    "csu": ("sbuf", [128, 8], U16),
    "last": ("sbuf", [128, TC], F32),
    "thr1": ("sbuf", [1, 16], I32), "thri": ("sbuf", [128, 16], I32),
    "thrf": ("sbuf", [128, 16], F32), "thrp": ("sbuf", [128, 16], F32),
    "j0": ("sbuf", [128, 16], I32), "jt": ("sbuf", [128, 16], I32), "turn": ("sbuf", [128, 16], U16),
    "colf": ("sbuf", [128, 12], F32),
    "jc": ("sbuf", [128, (R - 1) * TC], F32),
    "ent": ("sbuf", [128, N + 1], F32), "base": ("sbuf", [128, R * (N + 1)], F32),
    "cdo": ("sbuf", [128, LC], U16), "cso": ("sbuf", [128, LC], U16),
    "vrow": ("sbuf", [128, NB], F32), "vro2": ("sbuf", [128, NB], F32),
    "gr": ("sbuf", [128, WIN + K], F32), "keys": ("sbuf", [128, WIN], F32),
    "srow": ("sbuf", [128, K], U16), "trow": ("sbuf", [128, K], F32),
    "nl": ("sbuf", [128, 16 * R], U16), "bl": ("sbuf", [128, TC * R], F32),
    "both": ("sbuf", [128, 2 * (R - 1) * TC], F32),
    "zeros": ("sbuf", [128, 8], U16),
    "bit": ("sbuf", [128, NEW], "bfloat16"),
    "num": ("sbuf", [128, 4 * R], F32),
    "dec": ("sbuf", [128, 4 * R], F32),
    "uc": ("sbuf", [128, 128], CODE), "us": ("sbuf", [128, 128], BYTE),
    "vc": ("sbuf", [128, 128], CODE), "vs": ("sbuf", [128, 128], BYTE),
    "wc": ("sbuf", [128, 128 * R * O], CODE), "ws": ("sbuf", [128, 128 * R * O], BYTE),
    "xc": ("sbuf", [128, K], CODE), "xs": ("sbuf", [128, K], BYTE),
    "ty": ("sbuf", [128, R * O * K], F32),
    "acc": ("psum", [128, 1024], F32),
    "prod": ("psum", [128, 2048], F32),
}
for _t in range(R + 1):
    for _n, _d in (("c", CODE), ("s", BYTE)):
        SCRATCH["l%s%d" % (_n, _t)] = ("sbuf", [128, END if _t < R else K], _d)
        if _t < R:
            SCRATCH["s%s%d" % (_n, _t)] = ("sbuf", [128, 160], _d)
            SCRATCH["b%s%d" % (_n, _t)] = ("sbuf", [128, PAIRS + (K if _t == R - 1 else 0)], _d)
        if 0 < _t < R:
            SCRATCH["p%s%d" % (_n, _t)] = ("sbuf", [128, 2 * B], _d)
for _t in range(R):
    SCRATCH["pof%d" % _t] = ("sbuf", [128, 2], U16)
    SCRATCH["tl%d" % _t] = ("sbuf", [128, TC], U16)
    SCRATCH["pk%d" % _t] = ("sbuf", [128, N + 2], U16)

SEMAPHORES = ["vq", "aq", "pq", "gq", "lx0", "lx1", "lcs", "lcd", "lu", "lt", "yp", "lcn", "lo", "left", "begun"]
for _t in range(R):
    SEMAPHORES += [_n + str(_t) for _n in ("ln", "lb", "arr", "yo", "lw") + ("par", "dec") * min(_t, 1)]


def roads(topo, cores, s):
    src = cores[s]
    here = topo.chip(src)
    way = lambda c: 2 if topo.mates(here, c) else 1 if topo.same_plane(here, c) else 0
    chips = sorted({topo.chip(c) for c in cores} - {here}, key=way)
    on = lambda c: sorted((d for d in range(len(cores)) if d != s and topo.chip(cores[d]) == c), key=lambda d: topo.die(cores[d]) == topo.die(src))
    bits = lambda es: sum(1 << e for e in es)
    (near,), (partner, second) = on(here), on(chips[0 if FAR else -1])
    out = topo.engines(src, cores[partner])
    share = lambda ds: {d: bits(out[i::len(ds)]) for i, d in enumerate(ds)}
    first = [share(on(c)) for c in chips]
    later = [share([d for d in on(c) if d != partner]) for c in chips]
    first[1][near] = later[1][near] = bits([e for e in topo.engines(src, cores[near]) if e not in out])
    return {"first": first, "later": later, "partner": partner, "out": bits(out)}


def landing(road, d, s, t):
    turn = [(road[d]["partner"] + i) % N for i in range(N)]
    turn.remove(d)
    return K + (PAD if t else 0) + B * turn.index(s)


def rank_program(g, core, T, topo):
    r = T.rank_of(core)
    if r is None:
        return
    cores = list(T.cores)
    road = [roads(topo, cores, s) for s in range(N)]
    A, F = AluOpType, ActivationFunctionType
    me = road[r]
    mate = me["partner"]
    ones = lambda m: bin(m).count("1")

    total, W, RD = {}, {}, {}
    qs = {}
    for name, eng, sem in (("v", g.vector, "vq"), ("a", g.scalar, "aq"), ("p", g.tensor, "pq"), ("g", g, "gq"), ("s", g.sync, None)):
        qs[name] = {"eng": eng, "sem": sem, "seen": {}}

    def hold(q, toks):
        need = {}
        for sem, n in toks:
            n = total[sem] if n is None else n
            if qs[q]["seen"].get(sem, 0) < n:
                need[sem] = max(need.get(sem, 0), n)
        for sem in sorted(need, key=lambda s: (s[:3] in ("arr", "par", "dec"), s)):
            qs[q]["eng"].wait_ge(T.sem[sem], need[sem])
            qs[q]["seen"][sem] = need[sem]

    def order(q, rd, wr):
        toks = []
        for k in rd:
            toks += W[k]
        for k in wr:
            toks += W.get(k, []) + RD.get(k, [])
        hold(q, toks)

    def note(tok, rd, wr):
        for k in rd:
            RD.setdefault(k, []).append(tok)
        for k in wr:
            W[k] = [tok]
            RD[k] = []

    def do(q, make, rd, wr):
        order(q, rd, wr)
        sem = qs[q]["sem"]
        make(qs[q]["eng"]).then_inc(T.sem[sem], 1)
        total[sem] = total.get(sem, 0) + 1
        note((sem, total[sem]), rd, wr)

    def dma(q, sem, out, in_, rd, wr):
        order(q, rd, [])
        qs[q]["eng"].dma_start(out, in_).then_inc(T.sem[sem], 16)
        total[sem] = total.get(sem, 0) + 16
        tok = (sem, None)
        for k in rd:
            RD.setdefault(k, []).append(tok)
        for k in wr:
            if tok not in W.setdefault(k, []):
                W[k].append(tok)

    def ts(out, in0, s1, op0, rd, wr, s2=None, op1=None):
        if op1 is None:
            do("v", lambda e: e.tensor_scalar(out, in0, s1, None, op0), rd, wr)
        else:
            do("v", lambda e: e.tensor_scalar(out, in0, s1, s2, op0, op1), rd, wr)

    def cp(out, in_, rd, wr):
        do("v", lambda e: e.tensor_copy(out, in_), rd, wr)

    def act(out, in_, rd, wr, func=F.Copy, **kw):
        do("a", lambda e: e.activation(out, in_, func, **kw), rd, wr)

    for t in range(R):
        total["arr%d" % t] = 2 * sum(ones(m[r]) for o in road for m in o["later" if t else "first"] if r in m)
        W["land%d" % t] = [("arr%d" % t, None)]
        if t:
            total["par%d" % t], total["dec%d" % t] = 2 * ones(road[mate]["out"]), ones(road[mate]["out"])
            W["pair%d" % t], W["dec%d" % t] = [("par%d" % t, None)], [("dec%d" % t, None)]

    h = 2 * K
    dma("s", "lx0", T.xt[:, 0:h], T.x[:, 0:h], [], ["x0"])
    for i in range(8):
        dma("a" if i < 5 else "s", "lcs", T.csl[16 * i:16 * i + 16, :], T.cs[:, 0:LC], [], ["cs"])
    dma("s", "lx1", T.xt[:, h:2 * h], T.x[:, h:2 * h], [], ["x1"])
    for i in range(8):
        t = min(i, R - 1)
        dma("as"[i % 2], "lcd", T.cdg[16 * i:16 * i + 16, :], T.cd[:, LC * t:LC * t + LC], [], ["cd"])
    for i in range(8):
        src = T.cs[:, LC * (i + 1):LC * (i + 2)] if i < R - 1 else T.cd[:, LC * (R - 1):LC * R]
        dma("as"[i % 2], "lcn", T.csg[16 * i:16 * i + 16, :], src, [], ["csg"])
    dma("a", "lt", T.thr1[0:1, :], T.thr[:, :], [], ["thr1"])
    dma("s", "lu", T.ut[:, 0:8], T.u[:, 0:8], [], ["u"])

    fl = {"allow_small_or_imprecise_dtypes": True}
    row = T.gr[:, 0:WIN]
    lead = 16 * (2 * B * mate // 16 % 2)
    mine = (lead + 2 * B * mate) // 16
    do("g", lambda e: e.iota(T.j0[:, :], [[1, 16]], 0, 16), [], ["j0"])
    do("g", lambda e: e.iota(T.keys[:, 0:WIN // 2], [[1, WIN // 2]], 0, 0, **fl), [], ["keya"])
    runs = []
    for s in range(N):
        at = None if s == r else landing(road, r, s, 0) - B * s
        if runs and at in (None, runs[-1][2]):
            runs[-1][1] = s + 1
        elif runs and runs[-1][2] is None:
            runs[-1][1:] = [s + 1, at]
        else:
            runs.append([s, s + 1, at])
    for a, b, at in runs:
        do("g", lambda e: e.iota(T.vrow[:, B * a:B * b], [[1, B * (b - a)]], at + B * a, 0, **fl), [], ["vrow%d" % a])
    do("v", lambda e: e.memset(T.ut[:, 8:512], 0.0), [], ["u0"])
    do("v", lambda e: e.memset(T.gr[:, WIN + lead + 2 * NB:], 0.0), [], ["rest"])
    W["lead"] = []
    if lead:
        do("v", lambda e: e.memset(T.gr[:, WIN:WIN + lead], 0.0), [], ["lead"])
    p16, back, p16x, cap, late, pm, pq = (T.colf[:, i:i + 1] for i in range(7))
    ts(T.jt[:, :], T.j0[:, :], K - 1, A.bitwise_and, ["j0"], ["jt"])
    ts(late, T.j0[:, 0:1], float(K), A.is_ge, ["j0"], ["late"], float(PAD), A.mult)
    q16 = T.jt[:, 0:1]
    cp(T.turn[:, :], T.jt[:, :], ["jt"], ["turn"])
    ts(cap, q16, 1.0 / 16, A.mult, ["jt"], ["cap"], float(K), A.add)
    own = {}
    for c in range(LC):
        lo, hi = max(B * r - 16 * c, 0), min(B * r + B - 16 * c, 16)
        if lo < hi:
            own[c] = T.colf[:, 8 + len(own):9 + len(own)]
            ts(own[c], q16, 8.0 - 16 * (lo or hi), A.add, ["jt"], ["own%d" % c], K / 4.0 * (1 if lo else -1), A.mult)
    act(T.keys[:, WIN // 2:], T.keys[:, 0:WIN // 2], ["keya"], ["keys"], F.Identity, bias=float(WIN // 2))
    act(T.vro2[TAIL:, :], T.keys[TAIL:, 0:NB], ["keya"], ["vro3"], F.Identity, bias=K + HEAD + lead + (SPAN // 2 + 1) / SPAN, scale=2.0)
    act(row, T.keys[:, :], ["keya", "keys"], ["row"])
    act(T.vro2[0:TAIL, :], T.vrow[0:TAIL, :], ["late"] + ["vrow%d" % a for a, _b, _c in runs], ["vro2"], F.Identity, bias=T.colf[0:TAIL, 4:5])

    def pick(nm, out, win, off, rd, wr):
        o, w = T[out[0] % nm][:, out[1]:out[2]], T[win[0] % nm][:, win[1]:win[2]]
        if nm == "c":
            do("v", lambda e: e.tensor_copy(o.bitcast(dt.uint32), w.bitcast(dt.uint32).indirect(off)), rd, wr)
        else:
            act(o, w.indirect(off), rd, wr)

    def write(d, mask, sem, src, dst):
        rid, pid, _ring = topo.addr(cores[d])
        return RemoteDMATransfer(dst_ids=[DstId(rid=rid, pnc=pid)], dma_engine_mask=mask, remote_sem=T.sem[sem], src=src, dst=dst), ones(mask)

    def cols(nm, name, a, n):
        v = T[name % nm][:, a:a + n]
        return v.bitcast(dt.uint8) if nm == "c" else v

    def call(moves, sem, rd):
        order("g", rd, [])
        g.remote_dma_fused([m for m, _n in moves], local_sem=T.sem[sem])
        total[sem] = total.get(sem, 0) + sum(n for _m, n in moves)

    def send(t, where):
        for m in me["later" if t else "first"]:
            for nm in "cs":
                moves = [write(d, m[d], "arr%d" % t, cols(nm, "s%%s%d" % t, where[d][0], B), cols(nm, "l%%s%d" % t, landing(road, d, r, t), B)) for d in m]
                call(moves, "begun" if t == 0 and m is me["first"][0] else "left", ["snd%s%d%d" % (nm, t, where[d][1]) for d in m])
        W["begun"] = [("begun", None)]

    held = lambda x, t: ["tab%s%d" % (x, t), "land%d" % t] + ["got%s%d" % (x, t)] * min(t, 1)

    def fetch(t, rd):
        a, b = 512 * O * t, 512 * O * (t + 1)
        dma("s", "lw%d" % t, T.wt[:, a:b], T.w[:, a:b], rd, ["w%d" % t])

    def pack(t):
        a, b = 128 * O * t, 128 * O * (t + 1)
        do("v", lambda e: e.quantize_mx(T.wc[:, a:b], T.ws[:, a:b], T.wt[:, 4 * a:4 * b]), ["w%d" % t], ["wq%d" % t])

    def unload(t):
        for o in range(O):
            i = O * t + o
            pb = 512 * (i % 4)
            (act if o else cp)(T.ty[:, K * i:K * i + K], T.prod[:, pb:pb + K], ["prod%d" % (i % 4)], ["ty%d" % i])

    def store(t, rd):
        y = slice(O * K * t, O * K * (t + 1))
        dma("s", "yo%d" % t, T.y[:, y], T.ty[:, y], ["ty%d" % (O * t), "ty%d" % (O * t + 1)] + rd, ["out%d" % t])

    def lists(t, rd):
        p = 16 * t if t < R - 1 else TAIL
        dma("s", "ln%d" % t, T.nl[:, 16 * t:16 * t + 16], T.srow[16 * t:16 * t + 8, :], ["srow"] + rd, ["nl%d" % t])
        dma("s", "lb%d" % t, T.bl[:, 16 * t:16 * t + 16], T.trow[p:p + 8, :], ["trow"], ["bl%d" % t])

    def ready(t):
        bl = T.bl[:, TC * t:TC * t + TC]
        if t < R - 1:
            act(T.both[:, 2 * TC * t + 1:2 * TC * (t + 1):2], bl, ["bl%d" % t, "botha"], ["bothb%d" % t])
        else:
            act(T.last[:, :], bl, ["bl%d" % t, "back"], ["last"], F.Identity, bias=back, scale=float(SPAN))

    for t in range(EARLY):
        fetch(t, [])
    far = sorted(me["first"][0])
    a, b = B * far[0] // 16, (B * far[-1] + B + 15) // 16
    H = K // 2
    for i in range(2):
        do("v", lambda e: e.quantize_mx(T.xc[:, H * i:H * i + H], T.xs[:, H * i:H * i + H], T.xt[:, 4 * H * i:4 * H * (i + 1)]), ["x%d" % i], ["xq%d" % i])
        if i == 0:
            cp(T.csu[:, 0:LC], T.csl[:, :], ["cs"], ["csu0"])
            if a % 2:
                cp(T.csu[:, LC:LC + b - a], T.csl[:, a:b], ["cs"], ["csu1"])
    where = {d: (32 + B * d, 1) for d in range(N)}
    where.update({d: (B * d - 16 * a, 0) for d in far})
    for i, (to, off, rd) in enumerate(((0, T.csu[:, LC:LC + b - a] if a % 2 else T.csu[:, a:b], "csu%d" % (a % 2)), (32, T.csu[:, 0:LC], "csu0"))):
        for nm in "cs":
            pick(nm, ("s%s0", to, to + (NB if i else 16 * (b - a))), ("x%s", 0, K), off, ["xq0", "xq1", rd], ["snd%s0%d" % (nm, i)])
    send(0, where)

    here = []
    for c in range(LC):
        if c in own:
            ts(T.cdo[:, c:c + 1], T.cdg[:, c:c + 1], own[c], A.max, ["cd", "own%d" % c, "cap"], ["cdo%d" % c], cap, A.min)
            here.append("cdo%d" % c)
    for a, b in ((0, min(own)), (max(own) + 1, LC)):
        if a < b:
            cp(T.cdo[:, a:b], T.cdg[:, a:b], ["cd"], ["cdo%d" % a])
            here.append("cdo%d" % a)
    cp(T.cso[:, :], T.csg[:, :], ["csg"], ["cso"])
    cp(row.indirect(T.cdo[:, :]), T.vro2[:, :], here + ["vro2", "vro3"], ["row"])
    a = WIN + lead
    act(T.gr[:, a:a + 2 * NB:2], T.keys[:, :].indirect(T.cso[:, :]), ["keys", "cso"], ["grow"])
    cp(T.gr[:, a + 1:a + 2 * NB:2], row.indirect(T.cso[:, :]), ["cso", "row"], ["grow"])
    act(T.trow[:, :], row.indirect(T.turn[:, :]), ["row", "turn"], ["trow"])
    cp(T.srow[:, :], T.gr[:, WIN:].indirect(T.turn[:, :]), ["grow", "lead", "rest", "turn"], ["srow"])
    lists(0, [])
    lists(1, ["begun"])
    fetch(EARLY, ["begun"])
    SEL, PC = N, N + 1
    do("g", lambda e: e.iota(T.ent[:, 0:N], [[2 * SPAN * B, N]], SPAN * (HEAD + lead), 0, **fl), [], ["enta"])
    do("g", lambda e: e.iota(T.jc[:, :], [[0, R - 1], [16, TC]], 0, 0, **fl), [], ["jc"])
    do("g", lambda e: e.partition_broadcast(T.thri[:, :], T.thr1[0:1, :], 128), ["thr1", "jc"], ["thri"])
    do("v", lambda e: e.memset(T.zeros[:, :], 0), [], ["zeros"])
    cp(p16x, q16, ["jt"], ["p16x"])
    do("v", lambda e: e.quantize_mx(T.uc[:, :], T.us[:, :], T.ut[:, :]), ["u", "u0"], ["uq"])
    ts(pm, q16, 16.0 * (B - 1), A.min, ["jt"], ["pm"], SPAN / 8.0, A.mult)
    for nm in "cs":
        pick(nm, ("v%s", 0, 128), ("u%s", 0, 128), T.zeros[:, :], ["uq", "zeros"], ["v" + nm])
    do("v", lambda e: e.quantize_mx(T.lc0[:, 0:K], T.ls0[:, 0:K], T.xt[:, :]), ["x0", "x1"], ["tabc0", "tabs0"])
    ts(T.thrf[:, :], T.thri[:, :], 2.0, A.mult, ["thri"], ["thrf"], float(-NEW), A.add)
    ts(T.thrp[:, :], T.thri[:, :], -2.0, A.mult, ["thri", "pm"], ["thrp"], pm, A.add)
    half = float(NEW + SPAN // 2 + 1)
    act(T.ent[:, SEL:PC], p16x, ["p16x"], ["entb"], F.Relu, bias=-2.0 * SPAN * (B - 1), scale=SPAN / 8.0)
    act(p16, p16x, ["p16x"], ["p16f"], scale=1.0 / 16)
    act(pq, p16x, ["p16x"], ["pq"], F.Relu, bias=-2.0 * PAD, scale=1.0 / 8)
    act(T.ent[:, :], T.ent[:, :], ["enta", "entb"], ["ent"], F.Identity, bias=half)
    act(T.both[:, 0:2 * (R - 1) * TC:2], T.jc[:, :], ["jc", "p16f"], ["botha"], F.Identity, bias=p16)
    act(back, T.thrf[:, R - 1:R], ["thrf"], ["back"], scale=-1.0)
    for t in range(R - 1):
        act(T.base[:, PC * t:PC * t + PC], T.ent[:, :], ["thrp", "ent"], ["base%d" % t], F.Identity, bias=T.thrp[:, t:t + 1])
    pack(0)
    pack(1)
    slot, picks = {}, []
    for ms in (me["later"][:1], me["later"][1:]):
        ds = [d for m in ms for d in m if d not in slot]
        a, b, to = min(ds) // 2 * 2, max(ds) + 1, 32 * len(picks)
        slot.update({d: (to + 16 * (d - a), len(picks)) for d in range(a, b) if d not in slot})
        picks.append((a, b, to))

    for t in range(R):
        n = t + 1
        end = END if t else END - PAD
        win = ("l%%s%d" % t, 0, END)
        sb = 512 * (t % 2)
        cnt = T.num[:, 4 * t:4 * t + 1]
        do("p", lambda e: e.matmul_mx(T.acc[:, sb:sb + 128], T.vc[:, :], T.vs[:, :], T["lc%d" % t][:, end - 128:end], T["ls%d" % t][:, end - 128:end], True, True), ["vc", "vs"] + held("c", t) + held("s", t), ["acc%d" % (t % 2)])
        first, tl = (0 if n < R else K), T["tl%d" % t]
        whole = 2 * LC + lead // 16
        cuts = ((mine, mine + 2, 0), (0, whole, HEAD)) if n < R else ((0, SPLIT, HEAD), (SPLIT, whole, HEAD + 16 * SPLIT))
        for h, nm in ((0, "c"), (0, "s"), (1, "c"), (1, "s")):
            if (h, nm) == (1, "s"):
                act(T.bit[:, :], T.acc[:, sb + 128 - NEW:sb + 128], ["acc%d" % (t % 2)], ["cnt%d" % t, "bit"], F.Sign, bias=TINY, accum_out=cnt)
            a, b, to = cuts[h]
            pick(nm, ("b%%s%d" % t, first + to, first + to + 16 * (b - a)), win, T.nl[:, 16 * t + a:16 * t + b], held(nm, t) + ["nl%d" % t], ["c%s%d%d" % (nm, t, h)])
        pairs = lambda x: ["c%s%d0" % (x, t), "c%s%d1" % (x, t)]
        if n < R:
            for nm in "cs":
                call([write(mate, me["out"], "par%d" % n, cols(nm, "b%%s%d" % t, 2 * B * mate % 16, 2 * B), cols(nm, "p%%s%d" % n, 0, 2 * B))], "left", ["c%s%d0" % (nm, t)])
            call([write(mate, me["out"], "dec%d" % n, cnt, T.dec[:, 4 * n:4 * n + 1])], "left", ["cnt%d" % t])
            pk = T["pk%d" % t]
            ts(pk[:, 0:PC], T.base[:, PC * t:PC * t + PC], cnt, A.add, ["base%d" % t, "cnt%d" % t], ["pk%d" % t], 1.0 / SPAN, A.mult)
            for i, (a, b, to) in enumerate(picks):
                for nm in "cs":
                    pick(nm, ("s%%s%d" % n, to, to + 16 * (b - a)), ("b%%s%d" % t, 0, PAIRS), pk[:, a:b], pairs(nm) + ["pk%d" % t], ["snd%s%d%d" % (nm, n, i)])
            send(n, slot)
            if t == 0:
                ready(0)
            pof = T["pof%d" % t][:, 0:1]
            cp(tl[:, :], T.both[:, 2 * TC * t:2 * TC * (t + 1)].indirect(pk[:, SEL:SEL + 1]), ["pk%d" % t, "botha", "bothb%d" % t], ["tl%d" % t])
            for nm in "cs":
                pick(nm, ("l%%s%d" % n, 0, K), win, tl[:, :], held(nm, t) + ["tl%d" % t], ["tab%s%d" % (nm, n)])
            ts(pof, T.dec[:, 4 * n:4 * n + 1], T.thrf[:, t:t + 1], A.is_ge, ["dec%d" % n, "thrf", "pq"], ["pof%d" % t], pq, A.add)
            for nm in "cs":
                pick(nm, ("l%%s%d" % n, K, K + 16), ("p%%s%d" % n, 0, 2 * B), pof, ["pair%d" % n, "pof%d" % t], ["got%s%d" % (nm, n)])
            under = ["pof%d" % t]
            if n + 1 < R:
                lists(n + 1, under)
            if n + EARLY < R:
                fetch(n + EARLY, under)
            if n + 1 == R:
                for nm in "cs":
                    dma("s", "lo", cols(nm, "b%%s%d" % n, 0, K), cols(nm, "l%%s%d" % n, 0, K), ["tab%s%d" % (nm, n)] + under, ["kept"])
            if t:
                store(t - 1, under)
            for o in range(O):
                i = O * t + o
                pb = 512 * (i % 4)
                do("p", lambda e: e.matmul_mx(T.prod[:, pb:pb + K], T.wc[:, 128 * i:128 * i + 128], T.ws[:, 128 * i:128 * i + 128], T["lc%d" % n][:, 0:K], T["ls%d" % n][:, 0:K], True, True), ["wq%d" % t, "tabc%d" % n, "tabs%d" % n], ["prod%d" % (i % 4)])
            ready(n)
            if n + 1 < R:
                pack(n + 1)
            unload(t)
            if n + 1 == R:
                store(t, [])
        else:
            ts(tl[:, :], T.last[:, :], cnt, A.add, ["last", "cnt%d" % t], ["tl%d" % t], 1.0 / SPAN, A.mult)
            for h in range(2):
                for nm in "cs":
                    pick(nm, ("l%%s%d" % n, H * h, H * h + H), ("b%%s%d" % t, 0, K + PAIRS), tl[:, TC // 2 * h:TC // 2 * (h + 1)], pairs(nm) + ["kept", "tl%d" % t], ["tab%s%d%d" % (nm, n, h)])
                for o in range(O):
                    i = O * t + o
                    pb = 512 * (2 * h + o)
                    do("p", lambda e: e.matmul_mx(T.prod[:, pb:pb + H], T.wc[:, 128 * i:128 * i + 128], T.ws[:, 128 * i:128 * i + 128], T["lc%d" % n][:, H * h:H * h + H], T["ls%d" % n][:, H * h:H * h + H], True, True), ["wq%d" % t, "tabc%d%d" % (n, h), "tabs%d%d" % (n, h)], ["prod%d" % (2 * h + o)])
            for h in range(2):
                for o in range(O):
                    a, pb = K * (O * t + o) + H * h, 512 * (2 * h + o)
                    y = slice(a, a + H)
                    (act if o else cp)(T.ty[:, y], T.prod[:, pb:pb + H], ["prod%d" % (2 * h + o)], ["tyz%d%d" % (h, o)])
                    q, sem = ("a", "yp") if o and h else ("s", "yo%d" % t)
                    dma(q, sem, T.y[:, y], T.ty[:, y], ["tyz%d%d" % (h, o)], ["outz%d%d" % (h, o)])

    last = {"yp": "a", "yo%d" % (R - 1): "s", "aq": "a", "vq": "v", "pq": "p"}
    for sem in sorted(total, key=lambda s: s == "yp"):
        if all(q["seen"].get(sem, 0) < total[sem] for q in qs.values()):
            hold(last.get(sem, "g"), [(sem, None)])
